import numpy as np
import ml_dtypes


def mxq(x, axis, fmt="e4m3"):
    dtype, down = {"e4m3": (ml_dtypes.float8_e4m3fn, 7), "e5m2": (ml_dtypes.float8_e5m2, 14)}[fmt]
    v = np.moveaxis(np.asarray(x, np.float32).astype(ml_dtypes.bfloat16).astype(np.float64), axis, -1)
    blocks = v.reshape(v.shape[:-1] + (-1, 32))
    amax = np.abs(blocks).max(-1, keepdims=True)
    byte = np.maximum(np.where(amax > 0, np.frexp(amax)[1] - 1 + 127, 0) - down, 1)
    scale = np.exp2(byte - 127.0)
    codes = (blocks / scale).astype(np.float32).astype(dtype).astype(np.float64)
    return np.moveaxis((codes * scale).reshape(v.shape), -1, axis)


WIDE = False


def mx_kscale(k):
    if not WIDE:
        return np.ones(k)
    levels = np.array([10, -10, 5, -5, 0])
    if k % 512:
        return np.exp2(np.random.permutation(np.resize(levels, k // 32))).repeat(32)
    a = np.empty((k // 512, 16))
    for p in range(k // 512):
        a[p, :8] = np.random.permutation(np.resize(levels, 8))
        for g in range(8):
            far = levels[np.abs(levels - a[p, g]) >= 10]
            a[p, g + 8] = far[np.random.randint(len(far))]
    return np.exp2(a.ravel()).repeat(32)


BF16 = ml_dtypes.bfloat16


def bf(x):
    return np.asarray(x, np.float32).astype(BF16)


def f64(x):
    return np.asarray(x).astype(np.float64)

def planes(Y):
    n, m = Y.shape
    b = f64(bf(Y)).reshape(n // 32, 32, m)
    amax = np.abs(b).max(1)
    byte = np.clip(np.where(amax > 0, np.frexp(amax)[1] - 1 + 127 - 7, 1), 1, 254)
    codes = (b * np.exp2(127.0 - byte)[:, None, :]).reshape(n, m).astype(np.float32).astype(ml_dtypes.float8_e4m3fn).view(np.uint8)
    words = codes.reshape(n // 512, 128, 4, m).transpose(0, 1, 3, 2)
    return np.ascontiguousarray(words), np.ascontiguousarray(byte.astype(np.uint8).reshape(n // 512, 16, m))


B, N, M, C = 2, 1024, 1024, 512


def silu(a):
    return a / (1.0 + np.exp(-a))


def setup_inputs():
    s = mx_kscale(N)
    g = mx_kscale(N)
    t = mx_kscale(M)
    return {
        "x": bf(np.random.standard_normal((B, N, C)) / s[:, None]),
        "z": bf(np.random.standard_normal((B, N, C)) * g[:, None]),
        "q": bf(np.random.standard_normal((B, N, C))),
        "u": bf(np.random.standard_normal((M, N)) / np.sqrt(N) * s[None, :] * t[:, None]),
        "uh": bf(np.random.standard_normal((M, N)) / np.sqrt(N) / g[None, :]),
        "h0": bf(np.random.standard_normal((M, C))),
        "v": bf(np.random.standard_normal((N, M)) / np.sqrt(M) / t[None, :]),
    }


def core(x, z, q, u, uh, h0, v):
    xs = mxq(f64(u), 1, "e4m3") @ mxq(f64(x), 1, "e4m3")
    zs = mxq(f64(uh), 1, "e4m3") @ mxq(f64(z), 1, "e4m3")
    h = f64(h0)[None, :, :] + np.abs(zs)
    p = xs * h
    r = mxq(f64(v), 1, "e4m3") @ mxq(p, 1, "e4m3")
    return silu(f64(q)) * r


def reference(x, z, q, u, uh, h0, v):
    R_out = core(x, z, q, u, uh, h0, v)
    words, scales = planes(np.moveaxis(R_out, 1, 0).reshape(1024, -1))
    return R_out, words, scales

@@ -1,0 +1,336 @@
+from contextlib import ExitStack
+
+import concourse.mybir as mybir
+from concourse.masks import make_identity
+
+F32 = mybir.dt.float32
+BF16 = mybir.dt.bfloat16
+U32 = mybir.dt.uint32
+I32 = mybir.dt.int32
+U8 = mybir.dt.uint8
+FP8X4 = mybir.dt.float8_e4m3fn_x4
+ACT = mybir.ActivationFunctionType
+ALU = mybir.AluOpType
+
+B, N, M, C = 2, 1024, 1024, 512
+FLOPS = 3 * 2 * B * N * M * C
+
+P = 128
+PACK = 4
+G = P * PACK
+NG = N // G
+CH = 128
+NCH = C // CH
+
+
+def tile_orchiddatadependentspectralconv_x1_kernel(tc, x, z, q, u, uh, h0, v, out_0, out_1, out_2):
+    nc = tc.nc
+    with ExitStack() as ctx:
+        keep = ctx.enter_context(tc.tile_pool(name="keep", bufs=1))
+        wraw = ctx.enter_context(tc.tile_pool(name="wraw", bufs=4))
+        sraw = ctx.enter_context(tc.tile_pool(name="sraw", bufs=4))
+        qraw = ctx.enter_context(tc.tile_pool(name="qraw", bufs=4))
+        stage = ctx.enter_context(tc.tile_pool(name="stage", bufs=3))
+        work = ctx.enter_context(tc.tile_pool(name="work", bufs=2))
+        gates = ctx.enter_context(tc.tile_pool(name="gates", bufs=3))
+        elem = ctx.enter_context(tc.tile_pool(name="elem", bufs=3))
+        psum = ctx.enter_context(tc.psum_pool(name="psum", bufs=2))
+
+        ident = keep.tile([P, P], F32, name="ident")
+        make_identity(nc, ident[:])
+        warm = keep.tile([P, 8], F32, name="warm")
+        nc.vector.memset(warm[:], 0.0)
+        nc.scalar.activation(out=warm[:], in_=warm[:], func=ACT.Silu)
+
+        weights = {"u": u, "uh": uh, "v": v}
+        signals = {"x": x, "z": z}
+        raw = {}
+        codes = {}
+        scales = {}
+        grouped = {}
+
+        def load_weight(w, g):
+            t_raw = wraw.tile([P, PACK, N], BF16, name="w_raw")
+            raw[w, g] = t_raw
+            view = weights[w][g * G : (g + 1) * G, :].rearrange("(p t) k -> p t k", t=PACK)
+            for h in (0, 1):
+                nc.sync.dma_start(out=t_raw[:, 2 * h : 2 * h + 2, :], in_=view[:, 2 * h : 2 * h + 2, :])
+
+        def load_signal(s, b, k):
+            t_raw = sraw.tile([P, PACK, C], BF16, name="s_raw")
+            raw[s, b, k] = t_raw
+            nc.sync.dma_start(
+                out=t_raw[:], in_=signals[s][b, k * G : (k + 1) * G, :].rearrange("(p t) c -> p t c", t=PACK)
+            )
+
+        h_in = keep.tile([P, NG, PACK, C], BF16, name="h_in")
+
+        def load_h(g):
+            nc.sync.dma_start(out=h_in[:, g, :, :], in_=h0[g * G : (g + 1) * G, :].rearrange("(p t) c -> p t c", t=PACK))
+
+        def load_q(b, g):
+            t_raw = qraw.tile([P, PACK, C], BF16, name="q_raw")
+            raw["q", b, g] = t_raw
+            nc.sync.dma_start(out=t_raw[:], in_=q[b, g * G : (g + 1) * G, :].rearrange("(p t) c -> p t c", t=PACK))
+
+        def operand(key):
+            if key not in codes:
+                codes[key] = keep.tile([P, NG, G], U32, align_bytes=64, name="codes_%s" % "_".join(map(str, key)))
+                scales[key] = keep.tile([P, NG, G], U8, align_bytes=64, name="scales_%s" % "_".join(map(str, key)))
+
+        def quantize(key, k, src):
+            operand(key)
+            nc.vector.quantize_mx(
+                out=codes[key][:, k, :].bitcast(FP8X4),
+                scales=scales[key][:, k, :],
+                in_=src[:].rearrange("p w t -> p (w t)"),
+            )
+
+        def turn(w, g, h):
+            words = raw[w, g][:].bitcast(F32)
+            for k in range(NG):
+                bank = psum.tile([P, 2, 2, P], F32, name="turned", tag="bank", bufs=4)
+                for t in range(2):
+                    for e in range(2):
+                        nc.tensor.transpose(
+                            bank[:, t, e, :], words[:, 2 * h + t, 2 * P * k + e : 2 * P * (k + 1) : 2], ident[:]
+                        )
+                if h == 0:
+                    grouped[w, g, k] = stage.tile([P, G, PACK], BF16, align_bytes=64, name="w_grouped", bufs=4)
+                dst = grouped[w, g, k][:].rearrange("p w t -> p (w t)").bitcast(F32)
+                nc.scalar.copy(
+                    out=dst[:, h * G : (h + 1) * G].rearrange("p (t m e) -> p t m e", t=2, e=2),
+                    in_=bank[:].rearrange("p t e m -> p t m e"),
+                )
+
+        def quantize_weight(w, g, k):
+            quantize((w, g), k, grouped[w, g, k])
+
+        def interleave(s, b, k, eng):
+            t_g = stage.tile([P, C, PACK], BF16, align_bytes=64, name="s_grouped")
+            grouped[s, b, k] = t_g
+            o = t_g[:].rearrange("p (c i) t -> p c t i", i=4)
+            i = raw[s, b, k][:].rearrange("p t (c i) -> p c t i", i=4)
+            if eng == "v":
+                nc.vector.tensor_copy(out=o, in_=i)
+            else:
+                nc.scalar.copy(out=o, in_=i)
+
+        def quantize_signal(s, b, k):
+            quantize((s, b), k, grouped[s, b, k])
+
+        live = {}
+
+        def transform(b, g, c, w, s, name):
+            acc = psum.tile([P, PACK, CH], F32, name=name)
+            cols = slice(c * CH, (c + 1) * CH)
+            for t in range(PACK):
+                rows = slice(t * P, (t + 1) * P)
+                for k in range(NG):
+                    nc.tensor.matmul_mx(
+                        out=acc[:, t, :],
+                        lhsT=codes[w, g][:, k, rows].bitcast(FP8X4),
+                        lhsT_scale=scales[w, g][:, k, rows],
+                        rhs=codes[s, b][:, k, cols].bitcast(FP8X4),
+                        rhs_scale=scales[s, b][:, k, cols],
+                        start=(k == 0),
+                        stop=(k == NG - 1),
+                    )
+            live[name, b, g, c] = acc
+
+        def absolute(b, g, c):
+            mag = elem.tile([P, PACK, CH], F32, name="mag")
+            nc.scalar.activation(out=mag[:], in_=live["zs", b, g, c][:], func=ACT.Abs)
+            live["mag", b, g, c] = mag
+
+        def filt(b, g, c):
+            h = elem.tile([P, PACK, CH], F32, name="h")
+            nc.vector.tensor_tensor(
+                out=h[:], in0=live["mag", b, g, c][:], in1=h_in[:, g, :, c * CH : (c + 1) * CH], op=ALU.add
+            )
+            live["h", b, g, c] = h
+
+        def product(b, g, c):
+            if c == 0:
+                grouped["p", b, g] = work.tile([P, C, PACK], BF16, align_bytes=64, name="p_grouped")
+            dst = grouped["p", b, g][:, c * CH : (c + 1) * CH, :]
+            nc.vector.tensor_tensor(
+                out=dst.rearrange("p (c i) t -> p c t i", i=4),
+                in0=live["xs", b, g, c][:].rearrange("p t (c i) -> p c t i", i=4),
+                in1=live["h", b, g, c][:].rearrange("p t (c i) -> p c t i", i=4),
+                op=ALU.mult,
+            )
+
+        def quantize_product(b, g):
+            quantize(("p", b), g, grouped["p", b, g])
+
+        def gate(b, g, h):
+            if h == 0:
+                live["gate", b, g] = gates.tile([P, PACK, C], F32, name="gate")
+            nc.scalar.activation(
+                out=live["gate", b, g][:, 2 * h : 2 * h + 2, :], in_=raw["q", b, g][:, 2 * h : 2 * h + 2, :], func=ACT.Silu
+            )
+
+        def back(b, g, t):
+            acc = psum.tile([P, C], F32, name="r", tag="bank", bufs=4)
+            rows = slice(t * P, (t + 1) * P)
+            for k in range(NG):
+                nc.tensor.matmul_mx(
+                    out=acc[:],
+                    lhsT=codes["v", g][:, k, rows].bitcast(FP8X4),
+                    lhsT_scale=scales["v", g][:, k, rows],
+                    rhs=codes["p", b][:, k, :].bitcast(FP8X4),
+                    rhs_scale=scales["p", b][:, k, :],
+                    start=(k == 0),
+                    stop=(k == NG - 1),
+                )
+            live["r", b, g, t] = acc
+
+        def gated(b, g, t):
+            if t == 0:
+                live["out", b, g] = work.tile([P, PACK, C], F32, name="o")
+            o = live["out", b, g]
+            nc.vector.tensor_tensor(
+                out=o[:, t, :], in0=live["r", b, g, t][:], in1=live["gate", b, g][:, t, :], op=ALU.mult
+            )
+
+        def store_result(b, g):
+            nc.sync.dma_start(
+                out=out_0[b, g * G : (g + 1) * G, :].rearrange("(p t) c -> p t c", t=PACK), in_=live["out", b, g][:]
+            )
+
+        def regroup(b, g, h, eng):
+            if h == 0:
+                grouped["o", b, g] = work.tile([P, C, PACK], BF16, align_bytes=64, name="o_grouped")
+            cols = slice(h * C // 2, (h + 1) * C // 2)
+            o = grouped["o", b, g][:, cols, :].rearrange("p (c i) t -> p c t i", i=4)
+            i = live["out", b, g][:, :, cols].rearrange("p t (c i) -> p c t i", i=4)
+            if eng == "v":
+                nc.vector.tensor_copy(out=o, in_=i)
+            else:
+                nc.scalar.copy(out=o, in_=i)
+
+        plane = {}
+
+        def quantize_result(b, g, h):
+            if h == 0:
+                plane["w", b, g] = work.tile([P, C], U32, align_bytes=64, name="o_codes")
+                plane["s", b, g] = work.tile([P, C], U8, align_bytes=64, name="o_scales")
+            cols = slice(h * C // 2, (h + 1) * C // 2)
+            nc.vector.quantize_mx(
+                out=plane["w", b, g][:, cols].bitcast(FP8X4),
+                scales=plane["s", b, g][:, cols],
+                in_=grouped["o", b, g][:, cols, :].rearrange("p w t -> p (w t)"),
+            )
+
+        def store_planes(b, g):
+            cols = slice(b * C, (b + 1) * C)
+            nc.sync.dma_start(
+                out=out_1[g, :, cols, :].bitcast(I32).rearrange("p c o -> p (c o)"), in_=plane["w", b, g][:].bitcast(I32)
+            )
+            for r in range(4):
+                nc.sync.dma_start(
+                    out=out_2[g, 4 * r : 4 * r + 4, cols].bitcast(I32),
+                    in_=plane["s", b, g][32 * r : 32 * r + 4, :].bitcast(I32),
+                )
+
+        load_signal("x", 0, 0)
+        load_signal("x", 0, 1)
+        load_weight("u", 0)
+        load_weight("uh", 0)
+        load_signal("z", 0, 0)
+        load_signal("z", 0, 1)
+        load_h(0)
+        load_weight("uh", 1)
+        load_weight("u", 1)
+        load_signal("z", 1, 0)
+        load_signal("z", 1, 1)
+        load_h(1)
+        load_signal("x", 1, 0)
+        load_signal("x", 1, 1)
+        load_weight("v", 0)
+        load_q(0, 0)
+        load_weight("v", 1)
+        load_q(0, 1)
+        load_q(1, 0)
+        load_q(1, 1)
+
+        interleave("x", 0, 0, "v")
+        interleave("x", 0, 1, "v")
+        quantize_signal("x", 0, 0)
+        quantize_signal("x", 0, 1)
+        turn("u", 0, 0)
+        turn("u", 0, 1)
+        turn("uh", 0, 0)
+        quantize_weight("u", 0, 0)
+        quantize_weight("u", 0, 1)
+        turn("uh", 0, 1)
+        interleave("z", 0, 0, "v")
+        interleave("z", 0, 1, "s")
+        quantize_weight("uh", 0, 0)
+        quantize_signal("z", 0, 0)
+        quantize_weight("uh", 0, 1)
+        quantize_signal("z", 0, 1)
+
+        side = {
+            0: [lambda: turn("uh", 1, 0)],
+            1: [lambda: turn("uh", 1, 1), lambda: turn("u", 1, 0)],
+            2: [lambda: quantize_weight("uh", 1, 0), lambda: quantize_weight("uh", 1, 1), lambda: turn("u", 1, 1), lambda: interleave("z", 1, 0, "v")],
+            3: [lambda: quantize_weight("u", 1, 0), lambda: interleave("z", 1, 1, "s"), lambda: quantize_weight("u", 1, 1), lambda: quantize_signal("z", 1, 0)],
+            4: [lambda: turn("v", 0, 0), lambda: interleave("x", 1, 0, "v")],
+            5: [lambda: interleave("x", 1, 1, "s"), lambda: quantize_signal("z", 1, 1), lambda: turn("v", 0, 1), lambda: quantize_signal("x", 1, 0)],
+            6: [lambda: turn("v", 1, 0), lambda: quantize_signal("x", 1, 1), lambda: gate(0, 0, 0)],
+            7: [lambda: turn("v", 1, 1), lambda: quantize_weight("v", 0, 0), lambda: quantize_weight("v", 0, 1), lambda: gate(0, 0, 1)],
+            8: [lambda: quantize_weight("v", 1, 0), lambda: quantize_weight("v", 1, 1), lambda: back(0, 0, 0), lambda: gate(0, 1, 0)],
+            9: [lambda: back(0, 0, 1), lambda: gated(0, 0, 0), lambda: back(0, 0, 2), lambda: gate(0, 1, 1)],
+            10: [lambda: gated(0, 0, 1), lambda: back(0, 0, 3), lambda: gated(0, 0, 2)],
+            11: [lambda: gated(0, 0, 3), lambda: store_result(0, 0), lambda: regroup(0, 0, 0, "s"), lambda: back(0, 1, 0), lambda: back(0, 1, 1)],
+            12: [lambda: regroup(0, 0, 1, "s"), lambda: gated(0, 1, 0), lambda: back(0, 1, 2), lambda: gated(0, 1, 1), lambda: gate(1, 0, 0)],
+            13: [lambda: quantize_result(0, 0, 0), lambda: back(0, 1, 3), lambda: gated(0, 1, 2), lambda: gated(0, 1, 3), lambda: store_result(0, 1), lambda: gate(1, 0, 1)],
+            14: [lambda: quantize_result(0, 0, 1), lambda: store_planes(0, 0), lambda: regroup(0, 1, 0, "s"), lambda: gate(1, 1, 0)],
+            15: [lambda: regroup(0, 1, 1, "s"), lambda: gate(1, 1, 1)],
+        }
+        chunks = [(b, g, c) for b in range(B) for g in range(NG) for c in range(NCH)]
+        def zs_step(i):
+            b, g, c = chunks[i]
+            transform(b, g, c, "uh", "z", "zs")
+            absolute(b, g, c)
+
+        zs_step(0)
+        for i, (b, g, c) in enumerate(chunks):
+            if i == 0:
+                filt(b, g, c)
+            if i + 1 < len(chunks):
+                zs_step(i + 1)
+            transform(b, g, c, "u", "x", "xs")
+            if i + 1 < len(chunks):
+                filt(*chunks[i + 1])
+            product(b, g, c)
+            for task in side.get(i, []):
+                task()
+            if c == NCH - 1:
+                quantize_product(b, g)
+        for t in range(4):
+            back(1, 0, t)
+        quantize_result(0, 1, 0)
+        gated(1, 0, 0)
+        gated(1, 0, 1)
+        quantize_result(0, 1, 1)
+        store_planes(0, 1)
+        gated(1, 0, 2)
+        gated(1, 0, 3)
+        store_result(1, 0)
+        regroup(1, 0, 0, "s")
+        regroup(1, 0, 1, "s")
+        for t in range(4):
+            back(1, 1, t)
+            gated(1, 1, t)
+        store_result(1, 1)
+        quantize_result(1, 0, 0)
+        quantize_result(1, 0, 1)
+        store_planes(1, 0)
+        regroup(1, 1, 0, "v")
+        regroup(1, 1, 1, "s")
+        quantize_result(1, 1, 0)
+        quantize_result(1, 1, 1)
+        store_planes(1, 1)

@@ -36,6 +36,8 @@ def tile_orchiddatadependentspectralconv_x1_kernel(tc, x, z, q, u, uh, h0, v, ou
         elem = ctx.enter_context(tc.tile_pool(name="elem", bufs=3))
         psum = ctx.enter_context(tc.psum_pool(name="psum", bufs=2))
 
+        ctx.enter_context(tc.manual_schedule())
+
         ident = keep.tile([P, P], F32, name="ident")
         make_identity(nc, ident[:])
         warm = keep.tile([P, 8], F32, name="warm")
@@ -86,31 +88,44 @@ def tile_orchiddatadependentspectralconv_x1_kernel(tc, x, z, q, u, uh, h0, v, ou
                 in_=src[:].rearrange("p w t -> p (w t)"),
             )
 
+        def load_weight_half(w, g, h):
+            if (w, g) not in raw:
+                raw[w, g] = wraw.tile([P, PACK, N], BF16, name="w_raw")
+            view = weights[w][g * G : (g + 1) * G, :].rearrange("(p t) k -> p t k", t=PACK)
+            nc.sync.dma_start(out=raw[w, g][:, 2 * h : 2 * h + 2, :], in_=view[:, 2 * h : 2 * h + 2, :])
+
+        banks = {}
+
         def turn(w, g, h):
             words = raw[w, g][:].bitcast(F32)
             for k in range(NG):
                 bank = psum.tile([P, 2, 2, P], F32, name="turned", tag="bank", bufs=4)
+                banks[w, g, h, k] = bank
                 for t in range(2):
                     for e in range(2):
                         nc.tensor.transpose(
                             bank[:, t, e, :], words[:, 2 * h + t, 2 * P * k + e : 2 * P * (k + 1) : 2], ident[:]
                         )
-                if h == 0:
+
+        def unpack(w, g, h):
+            for k in range(NG):
+                if (w, g, k) not in grouped:
                     grouped[w, g, k] = stage.tile([P, G, PACK], BF16, align_bytes=64, name="w_grouped", bufs=4)
                 dst = grouped[w, g, k][:].rearrange("p w t -> p (w t)").bitcast(F32)
                 nc.scalar.copy(
                     out=dst[:, h * G : (h + 1) * G].rearrange("p (t m e) -> p t m e", t=2, e=2),
-                    in_=bank[:].rearrange("p t e m -> p t m e"),
+                    in_=banks[w, g, h, k][:].rearrange("p t e m -> p t m e"),
                 )
 
         def quantize_weight(w, g, k):
             quantize((w, g), k, grouped[w, g, k])
 
-        def interleave(s, b, k, eng):
-            t_g = stage.tile([P, C, PACK], BF16, align_bytes=64, name="s_grouped")
-            grouped[s, b, k] = t_g
-            o = t_g[:].rearrange("p (c i) t -> p c t i", i=4)
-            i = raw[s, b, k][:].rearrange("p t (c i) -> p c t i", i=4)
+        def interleave(s, b, k, half, eng):
+            if (s, b, k) not in grouped:
+                grouped[s, b, k] = stage.tile([P, C, PACK], BF16, align_bytes=64, name="s_grouped")
+            cols = slice(half * C // 2, (half + 1) * C // 2)
+            o = grouped[s, b, k][:, cols, :].rearrange("p (c i) t -> p c t i", i=4)
+            i = raw[s, b, k][:, :, cols].rearrange("p t (c i) -> p c t i", i=4)
             if eng == "v":
                 nc.vector.tensor_copy(out=o, in_=i)
             else:
@@ -143,15 +158,15 @@ def tile_orchiddatadependentspectralconv_x1_kernel(tc, x, z, q, u, uh, h0, v, ou
             nc.scalar.activation(out=mag[:], in_=live["zs", b, g, c][:], func=ACT.Abs)
             live["mag", b, g, c] = mag
 
-        def filt(b, g, c):
+        def filt(b, g, c, eng):
             h = elem.tile([P, PACK, CH], F32, name="h")
-            nc.vector.tensor_tensor(
+            (nc.vector if eng == "v" else nc.gpsimd).tensor_tensor(
                 out=h[:], in0=live["mag", b, g, c][:], in1=h_in[:, g, :, c * CH : (c + 1) * CH], op=ALU.add
             )
             live["h", b, g, c] = h
 
         def product(b, g, c):
-            if c == 0:
+            if ("p", b, g) not in grouped:
                 grouped["p", b, g] = work.tile([P, C, PACK], BF16, align_bytes=64, name="p_grouped")
             dst = grouped["p", b, g][:, c * CH : (c + 1) * CH, :]
             nc.vector.tensor_tensor(
@@ -161,176 +176,384 @@ def tile_orchiddatadependentspectralconv_x1_kernel(tc, x, z, q, u, uh, h0, v, ou
                 op=ALU.mult,
             )
 
-        def quantize_product(b, g):
-            quantize(("p", b), g, grouped["p", b, g])
+        def half_cols(half):
+            return slice(half * C // 2, (half + 1) * C // 2)
+
+        def quantize_product(b, g, half):
+            cols = half_cols(half)
+            operand(("p", b))
+            nc.vector.quantize_mx(
+                out=codes["p", b][:, g, cols].bitcast(FP8X4),
+                scales=scales["p", b][:, g, cols],
+                in_=grouped["p", b, g][:, cols, :].rearrange("p w t -> p (w t)"),
+            )
 
         def gate(b, g, h):
-            if h == 0:
+            if ("gate", b, g) not in live:
                 live["gate", b, g] = gates.tile([P, PACK, C], F32, name="gate")
             nc.scalar.activation(
                 out=live["gate", b, g][:, 2 * h : 2 * h + 2, :], in_=raw["q", b, g][:, 2 * h : 2 * h + 2, :], func=ACT.Silu
             )
 
-        def back(b, g, t):
-            acc = psum.tile([P, C], F32, name="r", tag="bank", bufs=4)
-            rows = slice(t * P, (t + 1) * P)
-            for k in range(NG):
-                nc.tensor.matmul_mx(
-                    out=acc[:],
-                    lhsT=codes["v", g][:, k, rows].bitcast(FP8X4),
-                    lhsT_scale=scales["v", g][:, k, rows],
-                    rhs=codes["p", b][:, k, :].bitcast(FP8X4),
-                    rhs_scale=scales["p", b][:, k, :],
-                    start=(k == 0),
-                    stop=(k == NG - 1),
-                )
-            live["r", b, g, t] = acc
+        def back(b, g, half, pair):
+            acc = psum.tile([P, 2, C // 2], F32, name="r", tag="bank", bufs=4)
+            cols = half_cols(half)
+            for t in range(2):
+                rows = slice((2 * pair + t) * P, (2 * pair + t + 1) * P)
+                for k in range(NG):
+                    nc.tensor.matmul_mx(
+                        out=acc[:, t, :],
+                        lhsT=codes["v", g][:, k, rows].bitcast(FP8X4),
+                        lhsT_scale=scales["v", g][:, k, rows],
+                        rhs=codes["p", b][:, k, cols].bitcast(FP8X4),
+                        rhs_scale=scales["p", b][:, k, cols],
+                        start=(k == 0),
+                        stop=(k == NG - 1),
+                    )
+            live["r", b, g, half, pair] = acc
 
-        def gated(b, g, t):
-            if t == 0:
+        def gated(b, g, half, pair):
+            if ("out", b, g) not in live:
                 live["out", b, g] = work.tile([P, PACK, C], F32, name="o")
-            o = live["out", b, g]
+            cols = half_cols(half)
+            rows = slice(2 * pair, 2 * pair + 2)
             nc.vector.tensor_tensor(
-                out=o[:, t, :], in0=live["r", b, g, t][:], in1=live["gate", b, g][:, t, :], op=ALU.mult
+                out=live["out", b, g][:, rows, cols],
+                in0=live["r", b, g, half, pair][:],
+                in1=live["gate", b, g][:, rows, cols],
+                op=ALU.mult,
             )
 
-        def store_result(b, g):
+        def store_result(b, g, half):
+            cols = half_cols(half)
             nc.sync.dma_start(
-                out=out_0[b, g * G : (g + 1) * G, :].rearrange("(p t) c -> p t c", t=PACK), in_=live["out", b, g][:]
+                out=out_0[b, g * G : (g + 1) * G, cols].rearrange("(p t) c -> p t c", t=PACK),
+                in_=live["out", b, g][:, :, cols],
             )
 
         def regroup(b, g, h, eng):
-            if h == 0:
+            if ("o", b, g) not in grouped:
                 grouped["o", b, g] = work.tile([P, C, PACK], BF16, align_bytes=64, name="o_grouped")
             cols = slice(h * C // 2, (h + 1) * C // 2)
             o = grouped["o", b, g][:, cols, :].rearrange("p (c i) t -> p c t i", i=4)
             i = live["out", b, g][:, :, cols].rearrange("p t (c i) -> p c t i", i=4)
             if eng == "v":
                 nc.vector.tensor_copy(out=o, in_=i)
+            elif eng == "g":
+                nc.gpsimd.tensor_scalar(out=o, in0=i, scalar1=1.0, scalar2=1.0, op0=ALU.mult, op1=ALU.mult)
             else:
                 nc.scalar.copy(out=o, in_=i)
 
         plane = {}
+        o_scales = keep.tile([P, NG, B * C], U8, align_bytes=64, name="o_scales")
 
-        def quantize_result(b, g, h):
-            if h == 0:
+        def quantize_result(b, g, half):
+            if ("w", b, g) not in plane:
                 plane["w", b, g] = work.tile([P, C], U32, align_bytes=64, name="o_codes")
-                plane["s", b, g] = work.tile([P, C], U8, align_bytes=64, name="o_scales")
-            cols = slice(h * C // 2, (h + 1) * C // 2)
+            cols = slice(half * C // 2, (half + 1) * C // 2)
             nc.vector.quantize_mx(
                 out=plane["w", b, g][:, cols].bitcast(FP8X4),
-                scales=plane["s", b, g][:, cols],
+                scales=o_scales[:, g, b * C + half * C // 2 : b * C + (half + 1) * C // 2],
                 in_=grouped["o", b, g][:, cols, :].rearrange("p w t -> p (w t)"),
             )
 
-        def store_planes(b, g):
-            cols = slice(b * C, (b + 1) * C)
+        def store_planes(b, g, half):
+            cols = half_cols(half)
+            dst = slice(b * C + half * C // 2, b * C + (half + 1) * C // 2)
             nc.sync.dma_start(
-                out=out_1[g, :, cols, :].bitcast(I32).rearrange("p c o -> p (c o)"), in_=plane["w", b, g][:].bitcast(I32)
+                out=out_1[g, :, dst, :].bitcast(I32).rearrange("p c o -> p (c o)"),
+                in_=plane["w", b, g][:, cols].bitcast(I32),
             )
+
+        def store_scales():
             for r in range(4):
-                nc.sync.dma_start(
-                    out=out_2[g, 4 * r : 4 * r + 4, cols].bitcast(I32),
-                    in_=plane["s", b, g][32 * r : 32 * r + 4, :].bitcast(I32),
+                nc.scalar.dma_start(
+                    out=out_2[:, 4 * r : 4 * r + 4, :].bitcast(I32).rearrange("g q m -> q g m"),
+                    in_=o_scales[32 * r : 32 * r + 4, :, :].bitcast(I32),
                 )
 
-        load_signal("x", 0, 0)
-        load_signal("x", 0, 1)
-        load_weight("u", 0)
-        load_weight("uh", 0)
-        load_signal("z", 0, 0)
-        load_signal("z", 0, 1)
-        load_h(0)
-        load_weight("uh", 1)
-        load_weight("u", 1)
-        load_signal("z", 1, 0)
-        load_signal("z", 1, 1)
-        load_h(1)
-        load_signal("x", 1, 0)
-        load_signal("x", 1, 1)
-        load_weight("v", 0)
-        load_q(0, 0)
-        load_weight("v", 1)
-        load_q(0, 1)
-        load_q(1, 0)
-        load_q(1, 1)
-
-        interleave("x", 0, 0, "v")
-        interleave("x", 0, 1, "v")
-        quantize_signal("x", 0, 0)
-        quantize_signal("x", 0, 1)
-        turn("u", 0, 0)
-        turn("u", 0, 1)
-        turn("uh", 0, 0)
-        quantize_weight("u", 0, 0)
-        quantize_weight("u", 0, 1)
-        turn("uh", 0, 1)
-        interleave("z", 0, 0, "v")
-        interleave("z", 0, 1, "s")
-        quantize_weight("uh", 0, 0)
-        quantize_signal("z", 0, 0)
-        quantize_weight("uh", 0, 1)
-        quantize_signal("z", 0, 1)
-
-        side = {
-            0: [lambda: turn("uh", 1, 0)],
-            1: [lambda: turn("uh", 1, 1), lambda: turn("u", 1, 0)],
-            2: [lambda: quantize_weight("uh", 1, 0), lambda: quantize_weight("uh", 1, 1), lambda: turn("u", 1, 1), lambda: interleave("z", 1, 0, "v")],
-            3: [lambda: quantize_weight("u", 1, 0), lambda: interleave("z", 1, 1, "s"), lambda: quantize_weight("u", 1, 1), lambda: quantize_signal("z", 1, 0)],
-            4: [lambda: turn("v", 0, 0), lambda: interleave("x", 1, 0, "v")],
-            5: [lambda: interleave("x", 1, 1, "s"), lambda: quantize_signal("z", 1, 1), lambda: turn("v", 0, 1), lambda: quantize_signal("x", 1, 0)],
-            6: [lambda: turn("v", 1, 0), lambda: quantize_signal("x", 1, 1), lambda: gate(0, 0, 0)],
-            7: [lambda: turn("v", 1, 1), lambda: quantize_weight("v", 0, 0), lambda: quantize_weight("v", 0, 1), lambda: gate(0, 0, 1)],
-            8: [lambda: quantize_weight("v", 1, 0), lambda: quantize_weight("v", 1, 1), lambda: back(0, 0, 0), lambda: gate(0, 1, 0)],
-            9: [lambda: back(0, 0, 1), lambda: gated(0, 0, 0), lambda: back(0, 0, 2), lambda: gate(0, 1, 1)],
-            10: [lambda: gated(0, 0, 1), lambda: back(0, 0, 3), lambda: gated(0, 0, 2)],
-            11: [lambda: gated(0, 0, 3), lambda: store_result(0, 0), lambda: regroup(0, 0, 0, "s"), lambda: back(0, 1, 0), lambda: back(0, 1, 1)],
-            12: [lambda: regroup(0, 0, 1, "s"), lambda: gated(0, 1, 0), lambda: back(0, 1, 2), lambda: gated(0, 1, 1), lambda: gate(1, 0, 0)],
-            13: [lambda: quantize_result(0, 0, 0), lambda: back(0, 1, 3), lambda: gated(0, 1, 2), lambda: gated(0, 1, 3), lambda: store_result(0, 1), lambda: gate(1, 0, 1)],
-            14: [lambda: quantize_result(0, 0, 1), lambda: store_planes(0, 0), lambda: regroup(0, 1, 0, "s"), lambda: gate(1, 1, 0)],
-            15: [lambda: regroup(0, 1, 1, "s"), lambda: gate(1, 1, 1)],
-        }
         chunks = [(b, g, c) for b in range(B) for g in range(NG) for c in range(NCH)]
-        def zs_step(i):
-            b, g, c = chunks[i]
-            transform(b, g, c, "uh", "z", "zs")
-            absolute(b, g, c)
+        loads = [
+            ('z', 0, 0),
+            ('u', 0, 0),
+            ('u', 0, 1),
+            ('z', 0, 1),
+            ('uh', 0, 0),
+            ('uh', 0, 1),
+            ('uh', 1, 0),
+            ('u', 1, 0),
+            ('x', 0, 0),
+            ('x', 0, 1),
+            ('uh', 1, 1),
+            ('h', 0),
+            ('z', 1, 0),
+            ('z', 1, 1),
+            ('u', 1, 1),
+            ('v', 0, 0),
+            ('x', 1, 0),
+            ('v', 1, 0),
+            ('v', 0, 1),
+            ('h', 1),
+            ('x', 1, 1),
+            ('v', 1, 1),
+            ('q', 0, 1),
+            ('q', 1, 0),
+            ('q', 0, 0),
+            ('q', 1, 1),
+        ]
+        plan = [
+            ('I', 'z', 0, 1, 0, 'v'),
+            ('T', 'u', 0, 0),
+            ('I', 'z', 0, 0, 0, 's'),
+            ('TC', 'u', 0, 0),
+            ('I', 'z', 0, 1, 1, 'v'),
+            ('T', 'u', 0, 1),
+            ('I', 'z', 0, 0, 1, 'v'),
+            ('SQ', 'z', 0, 1),
+            ('TC', 'u', 0, 1),
+            ('T', 'uh', 0, 0),
+            ('WQ', 'u', 0, 0),
+            ('TC', 'uh', 0, 0),
+            ('T', 'uh', 0, 1),
+            ('T', 'uh', 1, 0),
+            ('SQ', 'z', 0, 0),
+            ('TC', 'uh', 0, 1),
+            ('WQ', 'u', 0, 1),
+            ('WQ', 'uh', 0, 0),
+            ('T', 'u', 1, 0),
+            ('WQ', 'uh', 0, 1),
+            ('Z', 0),
+            ('TC', 'uh', 1, 0),
+            ('I', 'x', 0, 0, 0, 's'),
+            ('TC', 'u', 1, 0),
+            ('Z', 1),
+            ('I', 'x', 0, 0, 1, 'v'),
+            ('I', 'x', 0, 1, 0, 'v'),
+            ('T', 'uh', 1, 1),
+            ('I', 'x', 0, 1, 1, 'v'),
+            ('SQ', 'x', 0, 0),
+            ('A', 1),
+            ('A', 0),
+            ('SQ', 'x', 0, 1),
+            ('TC', 'uh', 1, 1),
+            ('F', 1, 'v'),
+            ('Z', 2),
+            ('X', 1),
+            ('X', 0),
+            ('F', 0, 'v'),
+            ('A', 2),
+            ('Z', 3),
+            ('I', 'z', 1, 0, 0, 's'),
+            ('WQ', 'uh', 1, 0),
+            ('A', 3),
+            ('M', 1),
+            ('X', 2),
+            ('T', 'u', 1, 1),
+            ('F', 2, 'v'),
+            ('I', 'z', 1, 1, 0, 'v'),
+            ('WQ', 'uh', 1, 1),
+            ('T', 'v', 0, 0),
+            ('M', 0),
+            ('I', 'z', 1, 0, 1, 's'),
+            ('TC', 'u', 1, 1),
+            ('Z', 6),
+            ('F', 3, 'v'),
+            ('I', 'z', 1, 1, 1, 's'),
+            ('Z', 7),
+            ('SQ', 'z', 1, 0),
+            ('A', 6),
+            ('WQ', 'u', 1, 0),
+            ('I', 'x', 1, 0, 0, 'v'),
+            ('WQ', 'u', 1, 1),
+            ('X', 3),
+            ('T', 'v', 0, 1),
+            ('SQ', 'z', 1, 1),
+            ('M', 3),
+            ('A', 7),
+            ('TC', 'v', 0, 0),
+            ('TC', 'v', 0, 1),
+            ('Z', 12),
+            ('PQ', 0, 0, 0),
+            ('F', 7, 'v'),
+            ('M', 2),
+            ('Z', 4),
+            ('F', 6, 'v'),
+            ('A', 12),
+            ('I', 'x', 1, 0, 1, 's'),
+            ('X', 6),
+            ('X', 7),
+            ('Z', 5),
+            ('WQ', 'v', 0, 0),
+            ('WQ', 'v', 0, 1),
+            ('T', 'v', 1, 1),
+            ('I', 'x', 1, 1, 0, 's'),
+            ('A', 4),
+            ('F', 12, 'v'),
+            ('I', 'x', 1, 1, 1, 's'),
+            ('SQ', 'x', 1, 0),
+            ('T', 'v', 1, 0),
+            ('A', 5),
+            ('M', 6),
+            ('PQ', 0, 0, 1),
+            ('M', 7),
+            ('TC', 'v', 1, 1),
+            ('Z', 13),
+            ('F', 4, 'v'),
+            ('PQ', 0, 1, 1),
+            ('X', 4),
+            ('X', 5),
+            ('SQ', 'x', 1, 1),
+            ('Z', 14),
+            ('F', 5, 'v'),
+            ('M', 4),
+            ('M', 5),
+            ('A', 13),
+            ('X', 12),
+            ('TC', 'v', 1, 0),
+            ('A', 14),
+            ('F', 13, 'v'),
+            ('PQ', 0, 1, 0),
+            ('G', 0, 0, 0),
+            ('Z', 15),
+            ('R', 0, 0, 1, 0),
+            ('Z', 10),
+            ('X', 14),
+            ('A', 15),
+            ('WQ', 'v', 1, 0),
+            ('R', 0, 0, 1, 1),
+            ('M', 12),
+            ('R', 0, 0, 0, 0),
+            ('F', 14, 'v'),
+            ('O', 0, 0, 1, 0),
+            ('R', 0, 0, 0, 1),
+            ('G', 0, 1, 0),
+            ('F', 15, 'v'),
+            ('X', 10),
+            ('M', 14),
+            ('A', 10),
+            ('WQ', 'v', 1, 1),
+            ('O', 0, 0, 0, 0),
+            ('Z', 11),
+            ('F', 10, 'v'),
+            ('G', 0, 0, 1),
+            ('G', 1, 1, 0),
+            ('O', 0, 0, 1, 1),
+            ('R', 0, 1, 1, 0),
+            ('X', 15),
+            ('Z', 8),
+            ('A', 11),
+            ('R', 0, 1, 0, 0),
+            ('M', 10),
+            ('O', 0, 0, 0, 1),
+            ('ST', 0, 0, 1),
+            ('R', 0, 1, 1, 1),
+            ('F', 11, 'v'),
+            ('M', 15),
+            ('O', 0, 1, 1, 0),
+            ('PQ', 1, 1, 1),
+            ('G', 0, 1, 1),
+            ('X', 11),
+            ('C', 0, 0, 1, 's'),
+            ('O', 0, 1, 0, 0),
+            ('Z', 9),
+            ('A', 8),
+            ('OQ', 0, 0, 1),
+            ('O', 0, 1, 1, 1),
+            ('G', 1, 1, 1),
+            ('C', 0, 1, 1, 's'),
+            ('R', 0, 1, 0, 1),
+            ('M', 11),
+            ('C', 0, 0, 0, 's'),
+            ('SP', 0, 0, 1),
+            ('F', 8, 'v'),
+            ('O', 0, 1, 0, 1),
+            ('X', 13),
+            ('A', 9),
+            ('X', 8),
+            ('PQ', 1, 0, 1),
+            ('R', 1, 0, 1, 0),
+            ('M', 8),
+            ('X', 9),
+            ('M', 13),
+            ('F', 9, 'v'),
+            ('ST', 0, 0, 0),
+            ('ST', 0, 1, 0),
+            ('ST', 0, 1, 1),
+            ('C', 0, 1, 0, 's'),
+            ('R', 1, 1, 1, 0),
+            ('OQ', 0, 1, 1),
+            ('M', 9),
+            ('PQ', 1, 1, 0),
+            ('R', 1, 1, 1, 1),
+            ('OQ', 0, 1, 0),
+            ('O', 1, 1, 1, 1),
+            ('SP', 0, 1, 0),
+            ('G', 1, 0, 0),
+            ('OQ', 0, 0, 0),
+            ('SP', 0, 0, 0),
+            ('O', 1, 1, 1, 0),
+            ('PQ', 1, 0, 0),
+            ('R', 1, 0, 1, 1),
+            ('R', 1, 1, 0, 0),
+            ('R', 1, 1, 0, 1),
+            ('G', 1, 0, 1),
+            ('O', 1, 0, 1, 0),
+            ('O', 1, 0, 1, 1),
+            ('C', 1, 1, 1, 's'),
+            ('O', 1, 1, 0, 0),
+            ('R', 1, 0, 0, 1),
+            ('SP', 0, 1, 1),
+            ('O', 1, 1, 0, 1),
+            ('O', 1, 0, 0, 1),
+            ('ST', 1, 1, 1),
+            ('R', 1, 0, 0, 0),
+            ('C', 1, 0, 1, 's'),
+            ('O', 1, 0, 0, 0),
+            ('C', 1, 1, 0, 's'),
+            ('ST', 1, 0, 1),
+            ('OQ', 1, 1, 0),
+            ('ST', 1, 1, 0),
+            ('ST', 1, 0, 0),
+            ('SP', 1, 1, 0),
+            ('OQ', 1, 1, 1),
+            ('C', 1, 0, 0, 's'),
+            ('OQ', 1, 0, 1),
+            ('OQ', 1, 0, 0),
+            ('SP', 1, 1, 1),
+            ('SP', 1, 0, 1),
+            ('SP', 1, 0, 0),
+            ('SC',),
+        ]
 
-        zs_step(0)
-        for i, (b, g, c) in enumerate(chunks):
-            if i == 0:
-                filt(b, g, c)
-            if i + 1 < len(chunks):
-                zs_step(i + 1)
-            transform(b, g, c, "u", "x", "xs")
-            if i + 1 < len(chunks):
-                filt(*chunks[i + 1])
-            product(b, g, c)
-            for task in side.get(i, []):
-                task()
-            if c == NCH - 1:
-                quantize_product(b, g)
-        for t in range(4):
-            back(1, 0, t)
-        quantize_result(0, 1, 0)
-        gated(1, 0, 0)
-        gated(1, 0, 1)
-        quantize_result(0, 1, 1)
-        store_planes(0, 1)
-        gated(1, 0, 2)
-        gated(1, 0, 3)
-        store_result(1, 0)
-        regroup(1, 0, 0, "s")
-        regroup(1, 0, 1, "s")
-        for t in range(4):
-            back(1, 1, t)
-            gated(1, 1, t)
-        store_result(1, 1)
-        quantize_result(1, 0, 0)
-        quantize_result(1, 0, 1)
-        store_planes(1, 0)
-        regroup(1, 1, 0, "v")
-        regroup(1, 1, 1, "s")
-        quantize_result(1, 1, 0)
-        quantize_result(1, 1, 1)
-        store_planes(1, 1)
+        for key in loads:
+            if key[0] in ("u", "uh", "v"):
+                load_weight_half(*key)
+            elif key[0] == "h":
+                load_h(key[1])
+            elif key[0] == "q":
+                load_q(*key[1:])
+            else:
+                load_signal(*key)
+        run = {
+            "T": turn,
+            "TC": unpack,
+            "WQ": quantize_weight,
+            "I": interleave,
+            "SQ": quantize_signal,
+            "Z": lambda i: transform(*chunks[i], "uh", "z", "zs"),
+            "A": lambda i: absolute(*chunks[i]),
+            "X": lambda i: transform(*chunks[i], "u", "x", "xs"),
+            "F": lambda i, eng: filt(*chunks[i], eng),
+            "M": lambda i: product(*chunks[i]),
+            "PQ": quantize_product,
+            "G": gate,
+            "R": back,
+            "O": gated,
+            "ST": store_result,
+            "C": regroup,
+            "OQ": quantize_result,
+            "SP": store_planes,
+            "SC": store_scales,
+        }
+        for task in plan:
+            run[task[0]](*task[1:])

@@ -16,544 +16,329 @@ B, N, M, C = 2, 1024, 1024, 512
 FLOPS = 3 * 2 * B * N * M * C
 
 P = 128
-PACK = 4
-G = P * PACK
-NG = N // G
-CH = 128
-NCH = C // CH
+T = 4
+GROUP = P * T
+NG = N // GROUP
+CHUNK = P
+HALF = C // 2
+SCALE_ROWS = 4
 
 
 def tile_orchiddatadependentspectralconv_x1_kernel(tc, x, z, q, u, uh, h0, v, out_0, out_1, out_2):
     nc = tc.nc
+    signals = {"x": x, "z": z}
+    weights = {"u": u, "uh": uh, "v": v}
+
     with ExitStack() as ctx:
         keep = ctx.enter_context(tc.tile_pool(name="keep", bufs=1))
-        wraw = ctx.enter_context(tc.tile_pool(name="wraw", bufs=4))
-        sraw = ctx.enter_context(tc.tile_pool(name="sraw", bufs=4))
-        qraw = ctx.enter_context(tc.tile_pool(name="qraw", bufs=4))
-        stage = ctx.enter_context(tc.tile_pool(name="stage", bufs=3))
-        work = ctx.enter_context(tc.tile_pool(name="work", bufs=2))
-        gates = ctx.enter_context(tc.tile_pool(name="gates", bufs=3))
-        elem = ctx.enter_context(tc.tile_pool(name="elem", bufs=3))
+        weight_pool = ctx.enter_context(tc.tile_pool(name="weight_pool", bufs=4))
+        signal_pool = ctx.enter_context(tc.tile_pool(name="signal_pool", bufs=4))
+        gate_in_pool = ctx.enter_context(tc.tile_pool(name="gate_in_pool", bufs=4))
+        group_pool = ctx.enter_context(tc.tile_pool(name="group_pool", bufs=3))
+        result_pool = ctx.enter_context(tc.tile_pool(name="result_pool", bufs=2))
+        gate_pool = ctx.enter_context(tc.tile_pool(name="gate_pool", bufs=3))
+        filter_pool = ctx.enter_context(tc.tile_pool(name="filter_pool", bufs=3))
         psum = ctx.enter_context(tc.psum_pool(name="psum", bufs=2))
 
         ctx.enter_context(tc.manual_schedule())
 
         ident = keep.tile([P, P], F32, name="ident")
         make_identity(nc, ident[:])
-        warm = keep.tile([P, 8], F32, name="warm")
-        nc.vector.memset(warm[:], 0.0)
-        nc.scalar.activation(out=warm[:], in_=warm[:], func=ACT.Silu)
+        zero = keep.tile([P, 1], F32, name="zero")
+        nc.vector.memset(zero[:], 0.0)
+        nc.scalar.activation(out=zero[:], in_=zero[:], func=ACT.Silu)
 
-        weights = {"u": u, "uh": uh, "v": v}
-        signals = {"x": x, "z": z}
+        filters = keep.tile([P, NG, T, C], BF16, name="filters")
+        out_scales = keep.tile([P, NG, B * C], U8, align_bytes=64, name="out_scales")
+
         raw = {}
-        codes = {}
-        scales = {}
         grouped = {}
+        codes, scales = {}, {}
+        banks = {}
+        live = {}
+        out_codes = {}
 
-        def load_weight(w, g):
-            t_raw = wraw.tile([P, PACK, N], BF16, name="w_raw")
-            raw[w, g] = t_raw
-            view = weights[w][g * G : (g + 1) * G, :].rearrange("(p t) k -> p t k", t=PACK)
-            for h in (0, 1):
-                nc.sync.dma_start(out=t_raw[:, 2 * h : 2 * h + 2, :], in_=view[:, 2 * h : 2 * h + 2, :])
+        def row_words(rows):
+            return rows.rearrange("(p t) c -> p t c", t=T)
+
+        def block(g):
+            return slice(g * GROUP, (g + 1) * GROUP)
+
+        def half_columns(half):
+            return slice(half * HALF, (half + 1) * HALF)
+
+        def by_fours(tile_view):
+            return tile_view.rearrange("p (c i) t -> p c t i", i=4)
+
+        def by_fours_of_rows(tile_view):
+            return tile_view.rearrange("p t (c i) -> p c t i", i=4)
+
+        def load_weight(w, g, pair):
+            if (w, g) not in raw:
+                raw[w, g] = weight_pool.tile([P, T, N], BF16, name="weight_in")
+            ts = slice(2 * pair, 2 * pair + 2)
+            nc.sync.dma_start(out=raw[w, g][:, ts, :], in_=row_words(weights[w][block(g), :])[:, ts, :])
 
         def load_signal(s, b, k):
-            t_raw = sraw.tile([P, PACK, C], BF16, name="s_raw")
-            raw[s, b, k] = t_raw
-            nc.sync.dma_start(
-                out=t_raw[:], in_=signals[s][b, k * G : (k + 1) * G, :].rearrange("(p t) c -> p t c", t=PACK)
-            )
+            raw[s, b, k] = signal_pool.tile([P, T, C], BF16, name="signal_in")
+            nc.sync.dma_start(out=raw[s, b, k][:], in_=row_words(signals[s][b, block(k), :]))
 
-        h_in = keep.tile([P, NG, PACK, C], BF16, name="h_in")
+        def load_filter(g):
+            nc.sync.dma_start(out=filters[:, g, :, :], in_=row_words(h0[block(g), :]))
 
-        def load_h(g):
-            nc.sync.dma_start(out=h_in[:, g, :, :], in_=h0[g * G : (g + 1) * G, :].rearrange("(p t) c -> p t c", t=PACK))
+        def load_gate(b, g):
+            raw["q", b, g] = gate_in_pool.tile([P, T, C], BF16, name="gate_in")
+            nc.sync.dma_start(out=raw["q", b, g][:], in_=row_words(q[b, block(g), :]))
 
-        def load_q(b, g):
-            t_raw = qraw.tile([P, PACK, C], BF16, name="q_raw")
-            raw["q", b, g] = t_raw
-            nc.sync.dma_start(out=t_raw[:], in_=q[b, g * G : (g + 1) * G, :].rearrange("(p t) c -> p t c", t=PACK))
-
-        def operand(key):
+        def quantize(key, k, columns, grouped_tile):
             if key not in codes:
-                codes[key] = keep.tile([P, NG, G], U32, align_bytes=64, name="codes_%s" % "_".join(map(str, key)))
-                scales[key] = keep.tile([P, NG, G], U8, align_bytes=64, name="scales_%s" % "_".join(map(str, key)))
-
-        def quantize(key, k, src):
-            operand(key)
+                codes[key] = keep.tile([P, NG, GROUP], U32, align_bytes=64, name="codes_%s_%d" % key)
+                scales[key] = keep.tile([P, NG, GROUP], U8, align_bytes=64, name="scales_%s_%d" % key)
             nc.vector.quantize_mx(
-                out=codes[key][:, k, :].bitcast(FP8X4),
-                scales=scales[key][:, k, :],
-                in_=src[:].rearrange("p w t -> p (w t)"),
+                out=codes[key][:, k, columns].bitcast(FP8X4),
+                scales=scales[key][:, k, columns],
+                in_=grouped_tile[:, columns, :].rearrange("p w t -> p (w t)"),
             )
 
-        def load_weight_half(w, g, h):
-            if (w, g) not in raw:
-                raw[w, g] = wraw.tile([P, PACK, N], BF16, name="w_raw")
-            view = weights[w][g * G : (g + 1) * G, :].rearrange("(p t) k -> p t k", t=PACK)
-            nc.sync.dma_start(out=raw[w, g][:, 2 * h : 2 * h + 2, :], in_=view[:, 2 * h : 2 * h + 2, :])
-
-        banks = {}
-
-        def turn(w, g, h):
+        def turn(w, g, pair):
             words = raw[w, g][:].bitcast(F32)
             for k in range(NG):
                 bank = psum.tile([P, 2, 2, P], F32, name="turned", tag="bank", bufs=4)
-                banks[w, g, h, k] = bank
+                banks[w, g, pair, k] = bank
                 for t in range(2):
                     for e in range(2):
                         nc.tensor.transpose(
-                            bank[:, t, e, :], words[:, 2 * h + t, 2 * P * k + e : 2 * P * (k + 1) : 2], ident[:]
+                            bank[:, t, e, :], words[:, 2 * pair + t, 2 * P * k + e : 2 * P * (k + 1) : 2], ident[:]
                         )
 
-        def unpack(w, g, h):
+        def unpack(w, g, pair):
             for k in range(NG):
                 if (w, g, k) not in grouped:
-                    grouped[w, g, k] = stage.tile([P, G, PACK], BF16, align_bytes=64, name="w_grouped", bufs=4)
-                dst = grouped[w, g, k][:].rearrange("p w t -> p (w t)").bitcast(F32)
+                    grouped[w, g, k] = group_pool.tile([P, GROUP, T], BF16, align_bytes=64, name="weight_grouped", bufs=4)
+                words = grouped[w, g, k][:].rearrange("p w t -> p (w t)").bitcast(F32)
                 nc.scalar.copy(
-                    out=dst[:, h * G : (h + 1) * G].rearrange("p (t m e) -> p t m e", t=2, e=2),
-                    in_=banks[w, g, h, k][:].rearrange("p t e m -> p t m e"),
+                    out=words[:, pair * GROUP : (pair + 1) * GROUP].rearrange("p (t m e) -> p t m e", t=2, e=2),
+                    in_=banks[w, g, pair, k][:].rearrange("p t e m -> p t m e"),
                 )
 
         def quantize_weight(w, g, k):
-            quantize((w, g), k, grouped[w, g, k])
+            quantize((w, g), k, slice(0, GROUP), grouped[w, g, k])
 
-        def interleave(s, b, k, half, eng):
+        def interleave(s, b, k, half, copy):
             if (s, b, k) not in grouped:
-                grouped[s, b, k] = stage.tile([P, C, PACK], BF16, align_bytes=64, name="s_grouped")
-            cols = slice(half * C // 2, (half + 1) * C // 2)
-            o = grouped[s, b, k][:, cols, :].rearrange("p (c i) t -> p c t i", i=4)
-            i = raw[s, b, k][:, :, cols].rearrange("p t (c i) -> p c t i", i=4)
-            if eng == "v":
-                nc.vector.tensor_copy(out=o, in_=i)
-            else:
-                nc.scalar.copy(out=o, in_=i)
+                grouped[s, b, k] = group_pool.tile([P, C, T], BF16, align_bytes=64, name="signal_grouped")
+            columns = half_columns(half)
+            copy(
+                out=by_fours(grouped[s, b, k][:, columns, :]), in_=by_fours_of_rows(raw[s, b, k][:, :, columns])
+            )
 
         def quantize_signal(s, b, k):
-            quantize((s, b), k, grouped[s, b, k])
+            quantize((s, b), k, slice(0, C), grouped[s, b, k])
 
-        live = {}
+        def multiply_mx(out, weight, t, moving, columns):
+            rows = slice(t * P, (t + 1) * P)
+            for k in range(NG):
+                nc.tensor.matmul_mx(
+                    out=out,
+                    lhsT=codes[weight][:, k, rows].bitcast(FP8X4),
+                    lhsT_scale=scales[weight][:, k, rows],
+                    rhs=codes[moving][:, k, columns].bitcast(FP8X4),
+                    rhs_scale=scales[moving][:, k, columns],
+                    start=(k == 0),
+                    stop=(k == NG - 1),
+                )
 
-        def transform(b, g, c, w, s, name):
-            acc = psum.tile([P, PACK, CH], F32, name=name)
-            cols = slice(c * CH, (c + 1) * CH)
-            for t in range(PACK):
-                rows = slice(t * P, (t + 1) * P)
-                for k in range(NG):
-                    nc.tensor.matmul_mx(
-                        out=acc[:, t, :],
-                        lhsT=codes[w, g][:, k, rows].bitcast(FP8X4),
-                        lhsT_scale=scales[w, g][:, k, rows],
-                        rhs=codes[s, b][:, k, cols].bitcast(FP8X4),
-                        rhs_scale=scales[s, b][:, k, cols],
-                        start=(k == 0),
-                        stop=(k == NG - 1),
-                    )
-            live[name, b, g, c] = acc
+        def chunk_columns(c):
+            return slice(c * CHUNK, (c + 1) * CHUNK)
 
-        def absolute(b, g, c):
-            mag = elem.tile([P, PACK, CH], F32, name="mag")
-            nc.scalar.activation(out=mag[:], in_=live["zs", b, g, c][:], func=ACT.Abs)
-            live["mag", b, g, c] = mag
+        def transform(name, b, g, c, w, s):
+            banks[name, b, g, c] = psum.tile([P, T, CHUNK], F32, name=name)
+            for t in range(T):
+                multiply_mx(banks[name, b, g, c][:, t, :], (w, g), t, (s, b), chunk_columns(c))
 
-        def filt(b, g, c, eng):
-            h = elem.tile([P, PACK, CH], F32, name="h")
-            (nc.vector if eng == "v" else nc.gpsimd).tensor_tensor(
-                out=h[:], in0=live["mag", b, g, c][:], in1=h_in[:, g, :, c * CH : (c + 1) * CH], op=ALU.add
+        def transform_z(b, g, c):
+            transform("zs", b, g, c, "uh", "z")
+
+        def transform_x(b, g, c):
+            transform("xs", b, g, c, "u", "x")
+
+        def magnitude(b, g, c):
+            live["mag", b, g, c] = filter_pool.tile([P, T, CHUNK], F32, name="mag")
+            nc.scalar.activation(out=live["mag", b, g, c][:], in_=banks["zs", b, g, c][:], func=ACT.Abs)
+
+        def add_filter(b, g, c, tensor_tensor):
+            live["h", b, g, c] = filter_pool.tile([P, T, CHUNK], F32, name="h")
+            tensor_tensor(
+                out=live["h", b, g, c][:],
+                in0=live["mag", b, g, c][:],
+                in1=filters[:, g, :, chunk_columns(c)],
+                op=ALU.add,
             )
-            live["h", b, g, c] = h
 
-        def product(b, g, c):
+        def multiply(b, g, c):
             if ("p", b, g) not in grouped:
-                grouped["p", b, g] = work.tile([P, C, PACK], BF16, align_bytes=64, name="p_grouped")
-            dst = grouped["p", b, g][:, c * CH : (c + 1) * CH, :]
+                grouped["p", b, g] = result_pool.tile([P, C, T], BF16, align_bytes=64, name="p_grouped")
             nc.vector.tensor_tensor(
-                out=dst.rearrange("p (c i) t -> p c t i", i=4),
-                in0=live["xs", b, g, c][:].rearrange("p t (c i) -> p c t i", i=4),
-                in1=live["h", b, g, c][:].rearrange("p t (c i) -> p c t i", i=4),
+                out=by_fours(grouped["p", b, g][:, chunk_columns(c), :]),
+                in0=by_fours_of_rows(banks["xs", b, g, c][:]),
+                in1=by_fours_of_rows(live["h", b, g, c][:]),
                 op=ALU.mult,
             )
 
-        def half_cols(half):
-            return slice(half * C // 2, (half + 1) * C // 2)
-
         def quantize_product(b, g, half):
-            cols = half_cols(half)
-            operand(("p", b))
-            nc.vector.quantize_mx(
-                out=codes["p", b][:, g, cols].bitcast(FP8X4),
-                scales=scales["p", b][:, g, cols],
-                in_=grouped["p", b, g][:, cols, :].rearrange("p w t -> p (w t)"),
-            )
+            quantize(("p", b), g, half_columns(half), grouped["p", b, g])
 
-        def gate(b, g, h):
+        def gate(b, g, pair):
             if ("gate", b, g) not in live:
-                live["gate", b, g] = gates.tile([P, PACK, C], F32, name="gate")
+                live["gate", b, g] = gate_pool.tile([P, T, C], F32, name="gate")
+            ts = slice(2 * pair, 2 * pair + 2)
             nc.scalar.activation(
-                out=live["gate", b, g][:, 2 * h : 2 * h + 2, :], in_=raw["q", b, g][:, 2 * h : 2 * h + 2, :], func=ACT.Silu
+                out=live["gate", b, g][:, ts, :], in_=raw["q", b, g][:, ts, :], func=ACT.Silu, bias=zero[:]
             )
 
-        def back(b, g, half, pair):
-            acc = psum.tile([P, 2, C // 2], F32, name="r", tag="bank", bufs=4)
-            cols = half_cols(half)
+        def transform_back(b, g, half, pair):
+            banks["r", b, g, half, pair] = psum.tile([P, 2, HALF], F32, name="r", tag="bank", bufs=4)
             for t in range(2):
-                rows = slice((2 * pair + t) * P, (2 * pair + t + 1) * P)
-                for k in range(NG):
-                    nc.tensor.matmul_mx(
-                        out=acc[:, t, :],
-                        lhsT=codes["v", g][:, k, rows].bitcast(FP8X4),
-                        lhsT_scale=scales["v", g][:, k, rows],
-                        rhs=codes["p", b][:, k, cols].bitcast(FP8X4),
-                        rhs_scale=scales["p", b][:, k, cols],
-                        start=(k == 0),
-                        stop=(k == NG - 1),
-                    )
-            live["r", b, g, half, pair] = acc
+                out = banks["r", b, g, half, pair][:, t, :]
+                multiply_mx(out, ("v", g), 2 * pair + t, ("p", b), half_columns(half))
 
-        def gated(b, g, half, pair):
+        def apply_gate(b, g, half, pair):
             if ("out", b, g) not in live:
-                live["out", b, g] = work.tile([P, PACK, C], F32, name="o")
-            cols = half_cols(half)
-            rows = slice(2 * pair, 2 * pair + 2)
+                live["out", b, g] = result_pool.tile([P, T, C], F32, name="result")
+            ts = slice(2 * pair, 2 * pair + 2)
             nc.vector.tensor_tensor(
-                out=live["out", b, g][:, rows, cols],
-                in0=live["r", b, g, half, pair][:],
-                in1=live["gate", b, g][:, rows, cols],
+                out=live["out", b, g][:, ts, half_columns(half)],
+                in0=banks["r", b, g, half, pair][:],
+                in1=live["gate", b, g][:, ts, half_columns(half)],
                 op=ALU.mult,
             )
 
         def store_result(b, g, half):
-            cols = half_cols(half)
-            nc.sync.dma_start(
-                out=out_0[b, g * G : (g + 1) * G, cols].rearrange("(p t) c -> p t c", t=PACK),
-                in_=live["out", b, g][:, :, cols],
+            columns = half_columns(half)
+            nc.sync.dma_start(out=row_words(out_0[b, block(g), columns]), in_=live["out", b, g][:, :, columns])
+
+        def regroup(b, g, half, copy):
+            if ("out", b, g) not in grouped:
+                grouped["out", b, g] = result_pool.tile([P, C, T], BF16, align_bytes=64, name="out_grouped")
+            columns = half_columns(half)
+            copy(
+                out=by_fours(grouped["out", b, g][:, columns, :]),
+                in_=by_fours_of_rows(live["out", b, g][:, :, columns]),
             )
-
-        def regroup(b, g, h, eng):
-            if ("o", b, g) not in grouped:
-                grouped["o", b, g] = work.tile([P, C, PACK], BF16, align_bytes=64, name="o_grouped")
-            cols = slice(h * C // 2, (h + 1) * C // 2)
-            o = grouped["o", b, g][:, cols, :].rearrange("p (c i) t -> p c t i", i=4)
-            i = live["out", b, g][:, :, cols].rearrange("p t (c i) -> p c t i", i=4)
-            if eng == "v":
-                nc.vector.tensor_copy(out=o, in_=i)
-            elif eng == "g":
-                nc.gpsimd.tensor_scalar(out=o, in0=i, scalar1=1.0, scalar2=1.0, op0=ALU.mult, op1=ALU.mult)
-            else:
-                nc.scalar.copy(out=o, in_=i)
-
-        plane = {}
-        o_scales = keep.tile([P, NG, B * C], U8, align_bytes=64, name="o_scales")
 
         def quantize_result(b, g, half):
-            if ("w", b, g) not in plane:
-                plane["w", b, g] = work.tile([P, C], U32, align_bytes=64, name="o_codes")
-            cols = slice(half * C // 2, (half + 1) * C // 2)
+            if (b, g) not in out_codes:
+                out_codes[b, g] = result_pool.tile([P, C], U32, align_bytes=64, name="out_codes")
+            columns = half_columns(half)
+            first = b * C + half * HALF
             nc.vector.quantize_mx(
-                out=plane["w", b, g][:, cols].bitcast(FP8X4),
-                scales=o_scales[:, g, b * C + half * C // 2 : b * C + (half + 1) * C // 2],
-                in_=grouped["o", b, g][:, cols, :].rearrange("p w t -> p (w t)"),
+                out=out_codes[b, g][:, columns].bitcast(FP8X4),
+                scales=out_scales[:, g, first : first + HALF],
+                in_=grouped["out", b, g][:, columns, :].rearrange("p w t -> p (w t)"),
             )
 
-        def store_planes(b, g, half):
-            cols = half_cols(half)
-            dst = slice(b * C + half * C // 2, b * C + (half + 1) * C // 2)
+        def store_codes(b, g, half):
+            first = b * C + half * HALF
             nc.sync.dma_start(
-                out=out_1[g, :, dst, :].bitcast(I32).rearrange("p c o -> p (c o)"),
-                in_=plane["w", b, g][:, cols].bitcast(I32),
+                out=out_1[g, :, first : first + HALF, :].bitcast(I32).rearrange("p c o -> p (c o)"),
+                in_=out_codes[b, g][:, half_columns(half)].bitcast(I32),
             )
 
         def store_scales():
-            for r in range(4):
+            for j in range(P // 32):
                 nc.scalar.dma_start(
-                    out=out_2[:, 4 * r : 4 * r + 4, :].bitcast(I32).rearrange("g q m -> q g m"),
-                    in_=o_scales[32 * r : 32 * r + 4, :, :].bitcast(I32),
+                    out=out_2[:, SCALE_ROWS * j : SCALE_ROWS * (j + 1), :].bitcast(I32).rearrange("g r m -> r g m"),
+                    in_=out_scales[32 * j : 32 * j + SCALE_ROWS, :, :].bitcast(I32),
                 )
 
-        chunks = [(b, g, c) for b in range(B) for g in range(NG) for c in range(NCH)]
         loads = [
-            ('z', 0, 0),
-            ('u', 0, 0),
-            ('u', 0, 1),
-            ('z', 0, 1),
-            ('uh', 0, 0),
-            ('uh', 0, 1),
-            ('uh', 1, 0),
-            ('u', 1, 0),
-            ('x', 0, 0),
-            ('x', 0, 1),
-            ('uh', 1, 1),
-            ('h', 0),
-            ('z', 1, 0),
-            ('z', 1, 1),
-            ('u', 1, 1),
-            ('v', 0, 0),
-            ('x', 1, 0),
-            ('v', 1, 0),
-            ('v', 0, 1),
-            ('h', 1),
-            ('x', 1, 1),
-            ('v', 1, 1),
-            ('q', 0, 1),
-            ('q', 1, 0),
-            ('q', 0, 0),
-            ('q', 1, 1),
-        ]
-        plan = [
-            ('I', 'z', 0, 1, 0, 'v'),
-            ('T', 'u', 0, 0),
-            ('I', 'z', 0, 0, 0, 's'),
-            ('TC', 'u', 0, 0),
-            ('I', 'z', 0, 1, 1, 'v'),
-            ('T', 'u', 0, 1),
-            ('I', 'z', 0, 0, 1, 'v'),
-            ('SQ', 'z', 0, 1),
-            ('TC', 'u', 0, 1),
-            ('T', 'uh', 0, 0),
-            ('WQ', 'u', 0, 0),
-            ('TC', 'uh', 0, 0),
-            ('T', 'uh', 0, 1),
-            ('T', 'uh', 1, 0),
-            ('SQ', 'z', 0, 0),
-            ('TC', 'uh', 0, 1),
-            ('WQ', 'u', 0, 1),
-            ('WQ', 'uh', 0, 0),
-            ('T', 'u', 1, 0),
-            ('WQ', 'uh', 0, 1),
-            ('Z', 0),
-            ('TC', 'uh', 1, 0),
-            ('I', 'x', 0, 0, 0, 's'),
-            ('TC', 'u', 1, 0),
-            ('Z', 1),
-            ('I', 'x', 0, 0, 1, 'v'),
-            ('I', 'x', 0, 1, 0, 'v'),
-            ('T', 'uh', 1, 1),
-            ('I', 'x', 0, 1, 1, 'v'),
-            ('SQ', 'x', 0, 0),
-            ('A', 1),
-            ('A', 0),
-            ('SQ', 'x', 0, 1),
-            ('TC', 'uh', 1, 1),
-            ('F', 1, 'v'),
-            ('Z', 2),
-            ('X', 1),
-            ('X', 0),
-            ('F', 0, 'v'),
-            ('A', 2),
-            ('Z', 3),
-            ('I', 'z', 1, 0, 0, 's'),
-            ('WQ', 'uh', 1, 0),
-            ('A', 3),
-            ('M', 1),
-            ('X', 2),
-            ('T', 'u', 1, 1),
-            ('F', 2, 'v'),
-            ('I', 'z', 1, 1, 0, 'v'),
-            ('WQ', 'uh', 1, 1),
-            ('T', 'v', 0, 0),
-            ('M', 0),
-            ('I', 'z', 1, 0, 1, 's'),
-            ('TC', 'u', 1, 1),
-            ('Z', 6),
-            ('F', 3, 'v'),
-            ('I', 'z', 1, 1, 1, 's'),
-            ('Z', 7),
-            ('SQ', 'z', 1, 0),
-            ('A', 6),
-            ('WQ', 'u', 1, 0),
-            ('I', 'x', 1, 0, 0, 'v'),
-            ('WQ', 'u', 1, 1),
-            ('X', 3),
-            ('T', 'v', 0, 1),
-            ('SQ', 'z', 1, 1),
-            ('M', 3),
-            ('A', 7),
-            ('TC', 'v', 0, 0),
-            ('TC', 'v', 0, 1),
-            ('Z', 12),
-            ('PQ', 0, 0, 0),
-            ('F', 7, 'v'),
-            ('M', 2),
-            ('Z', 4),
-            ('F', 6, 'v'),
-            ('A', 12),
-            ('I', 'x', 1, 0, 1, 's'),
-            ('X', 6),
-            ('X', 7),
-            ('Z', 5),
-            ('WQ', 'v', 0, 0),
-            ('WQ', 'v', 0, 1),
-            ('T', 'v', 1, 1),
-            ('I', 'x', 1, 1, 0, 's'),
-            ('A', 4),
-            ('F', 12, 'v'),
-            ('I', 'x', 1, 1, 1, 's'),
-            ('SQ', 'x', 1, 0),
-            ('T', 'v', 1, 0),
-            ('A', 5),
-            ('M', 6),
-            ('PQ', 0, 0, 1),
-            ('M', 7),
-            ('TC', 'v', 1, 1),
-            ('Z', 13),
-            ('F', 4, 'v'),
-            ('PQ', 0, 1, 1),
-            ('X', 4),
-            ('X', 5),
-            ('SQ', 'x', 1, 1),
-            ('Z', 14),
-            ('F', 5, 'v'),
-            ('M', 4),
-            ('M', 5),
-            ('A', 13),
-            ('X', 12),
-            ('TC', 'v', 1, 0),
-            ('A', 14),
-            ('F', 13, 'v'),
-            ('PQ', 0, 1, 0),
-            ('G', 0, 0, 0),
-            ('Z', 15),
-            ('R', 0, 0, 1, 0),
-            ('Z', 10),
-            ('X', 14),
-            ('A', 15),
-            ('WQ', 'v', 1, 0),
-            ('R', 0, 0, 1, 1),
-            ('M', 12),
-            ('R', 0, 0, 0, 0),
-            ('F', 14, 'v'),
-            ('O', 0, 0, 1, 0),
-            ('R', 0, 0, 0, 1),
-            ('G', 0, 1, 0),
-            ('F', 15, 'v'),
-            ('X', 10),
-            ('M', 14),
-            ('A', 10),
-            ('WQ', 'v', 1, 1),
-            ('O', 0, 0, 0, 0),
-            ('Z', 11),
-            ('F', 10, 'v'),
-            ('G', 0, 0, 1),
-            ('G', 1, 1, 0),
-            ('O', 0, 0, 1, 1),
-            ('R', 0, 1, 1, 0),
-            ('X', 15),
-            ('Z', 8),
-            ('A', 11),
-            ('R', 0, 1, 0, 0),
-            ('M', 10),
-            ('O', 0, 0, 0, 1),
-            ('ST', 0, 0, 1),
-            ('R', 0, 1, 1, 1),
-            ('F', 11, 'v'),
-            ('M', 15),
-            ('O', 0, 1, 1, 0),
-            ('PQ', 1, 1, 1),
-            ('G', 0, 1, 1),
-            ('X', 11),
-            ('C', 0, 0, 1, 's'),
-            ('O', 0, 1, 0, 0),
-            ('Z', 9),
-            ('A', 8),
-            ('OQ', 0, 0, 1),
-            ('O', 0, 1, 1, 1),
-            ('G', 1, 1, 1),
-            ('C', 0, 1, 1, 's'),
-            ('R', 0, 1, 0, 1),
-            ('M', 11),
-            ('C', 0, 0, 0, 's'),
-            ('SP', 0, 0, 1),
-            ('F', 8, 'v'),
-            ('O', 0, 1, 0, 1),
-            ('X', 13),
-            ('A', 9),
-            ('X', 8),
-            ('PQ', 1, 0, 1),
-            ('R', 1, 0, 1, 0),
-            ('M', 8),
-            ('X', 9),
-            ('M', 13),
-            ('F', 9, 'v'),
-            ('ST', 0, 0, 0),
-            ('ST', 0, 1, 0),
-            ('ST', 0, 1, 1),
-            ('C', 0, 1, 0, 's'),
-            ('R', 1, 1, 1, 0),
-            ('OQ', 0, 1, 1),
-            ('M', 9),
-            ('PQ', 1, 1, 0),
-            ('R', 1, 1, 1, 1),
-            ('OQ', 0, 1, 0),
-            ('O', 1, 1, 1, 1),
-            ('SP', 0, 1, 0),
-            ('G', 1, 0, 0),
-            ('OQ', 0, 0, 0),
-            ('SP', 0, 0, 0),
-            ('O', 1, 1, 1, 0),
-            ('PQ', 1, 0, 0),
-            ('R', 1, 0, 1, 1),
-            ('R', 1, 1, 0, 0),
-            ('R', 1, 1, 0, 1),
-            ('G', 1, 0, 1),
-            ('O', 1, 0, 1, 0),
-            ('O', 1, 0, 1, 1),
-            ('C', 1, 1, 1, 's'),
-            ('O', 1, 1, 0, 0),
-            ('R', 1, 0, 0, 1),
-            ('SP', 0, 1, 1),
-            ('O', 1, 1, 0, 1),
-            ('O', 1, 0, 0, 1),
-            ('ST', 1, 1, 1),
-            ('R', 1, 0, 0, 0),
-            ('C', 1, 0, 1, 's'),
-            ('O', 1, 0, 0, 0),
-            ('C', 1, 1, 0, 's'),
-            ('ST', 1, 0, 1),
-            ('OQ', 1, 1, 0),
-            ('ST', 1, 1, 0),
-            ('ST', 1, 0, 0),
-            ('SP', 1, 1, 0),
-            ('OQ', 1, 1, 1),
-            ('C', 1, 0, 0, 's'),
-            ('OQ', 1, 0, 1),
-            ('OQ', 1, 0, 0),
-            ('SP', 1, 1, 1),
-            ('SP', 1, 0, 1),
-            ('SP', 1, 0, 0),
-            ('SC',),
+            (load_signal, "z", 0, 0), (load_signal, "z", 0, 1), (load_weight, "uh", 0, 0),
+            (load_weight, "uh", 0, 1), (load_weight, "u", 0, 0), (load_weight, "u", 0, 1),
+            (load_signal, "x", 0, 0), (load_weight, "uh", 1, 0), (load_weight, "uh", 1, 1),
+            (load_signal, "z", 1, 0), (load_signal, "x", 0, 1), (load_weight, "u", 1, 0),
+            (load_weight, "u", 1, 1), (load_filter, 0), (load_weight, "v", 0, 0), (load_weight, "v", 0, 1),
+            (load_signal, "x", 1, 0), (load_filter, 1), (load_signal, "z", 1, 1), (load_signal, "x", 1, 1),
+            (load_gate, 0, 1), (load_weight, "v", 1, 0), (load_weight, "v", 1, 1), (load_gate, 1, 0),
+            (load_gate, 1, 1), (load_gate, 0, 0),
         ]
 
-        for key in loads:
-            if key[0] in ("u", "uh", "v"):
-                load_weight_half(*key)
-            elif key[0] == "h":
-                load_h(key[1])
-            elif key[0] == "q":
-                load_q(*key[1:])
-            else:
-                load_signal(*key)
-        run = {
-            "T": turn,
-            "TC": unpack,
-            "WQ": quantize_weight,
-            "I": interleave,
-            "SQ": quantize_signal,
-            "Z": lambda i: transform(*chunks[i], "uh", "z", "zs"),
-            "A": lambda i: absolute(*chunks[i]),
-            "X": lambda i: transform(*chunks[i], "u", "x", "xs"),
-            "F": lambda i, eng: filt(*chunks[i], eng),
-            "M": lambda i: product(*chunks[i]),
-            "PQ": quantize_product,
-            "G": gate,
-            "R": back,
-            "O": gated,
-            "ST": store_result,
-            "C": regroup,
-            "OQ": quantize_result,
-            "SP": store_planes,
-            "SC": store_scales,
-        }
-        for task in plan:
-            run[task[0]](*task[1:])
+        work = [
+            (interleave, "z", 0, 0, 0, nc.vector.tensor_copy),
+            (interleave, "z", 0, 1, 0, nc.vector.tensor_copy),
+            (interleave, "z", 0, 0, 1, nc.vector.tensor_copy), (turn, "uh", 0, 0), (unpack, "uh", 0, 0),
+            (interleave, "z", 0, 1, 1, nc.vector.tensor_copy), (turn, "uh", 0, 1), (unpack, "uh", 0, 1),
+            (quantize_signal, "z", 0, 1), (turn, "u", 0, 0), (quantize_signal, "z", 0, 0),
+            (quantize_weight, "uh", 0, 0), (quantize_weight, "uh", 0, 1), (turn, "u", 0, 1),
+            (interleave, "x", 0, 0, 0, nc.vector.tensor_copy), (unpack, "u", 0, 0),
+            (interleave, "x", 0, 0, 1, nc.vector.tensor_copy), (transform_z, 0, 0, 0), (unpack, "u", 0, 1),
+            (transform_z, 0, 0, 2), (quantize_weight, "u", 0, 0),
+            (interleave, "z", 1, 0, 0, nc.vector.tensor_copy), (magnitude, 0, 0, 0),
+            (quantize_signal, "x", 0, 0), (turn, "uh", 1, 0), (quantize_weight, "u", 0, 1),
+            (interleave, "x", 0, 1, 0, nc.vector.tensor_copy), (turn, "uh", 1, 1), (transform_z, 0, 0, 3),
+            (magnitude, 0, 0, 2), (unpack, "uh", 1, 0), (transform_z, 0, 0, 1), (unpack, "uh", 1, 1),
+            (turn, "u", 1, 0), (interleave, "x", 0, 1, 1, nc.scalar.copy), (quantize_weight, "uh", 1, 0),
+            (quantize_weight, "uh", 1, 1), (turn, "u", 1, 1), (transform_z, 0, 1, 2), (turn, "v", 0, 0),
+            (magnitude, 0, 0, 1), (quantize_signal, "x", 0, 1), (add_filter, 0, 0, 0, nc.vector.tensor_tensor),
+            (unpack, "u", 1, 0), (magnitude, 0, 0, 3), (turn, "v", 0, 1),
+            (interleave, "z", 1, 0, 1, nc.vector.tensor_copy), (unpack, "u", 1, 1),
+            (add_filter, 0, 0, 3, nc.vector.tensor_tensor), (unpack, "v", 0, 0), (quantize_signal, "z", 1, 0),
+            (magnitude, 0, 1, 2), (quantize_weight, "u", 1, 0), (quantize_weight, "u", 1, 1),
+            (add_filter, 0, 1, 2, nc.gpsimd.tensor_tensor), (transform_x, 0, 0, 0), (transform_z, 0, 1, 0),
+            (interleave, "x", 1, 0, 0, nc.vector.tensor_copy), (interleave, "x", 1, 0, 1, nc.scalar.copy),
+            (transform_x, 0, 1, 2), (interleave, "z", 1, 1, 0, nc.scalar.copy), (transform_z, 0, 1, 3),
+            (multiply, 0, 0, 0), (transform_x, 0, 0, 3), (magnitude, 0, 1, 3),
+            (interleave, "z", 1, 1, 1, nc.vector.tensor_copy), (add_filter, 0, 0, 2, nc.gpsimd.tensor_tensor),
+            (unpack, "v", 0, 1), (transform_x, 0, 0, 2), (transform_z, 0, 1, 1), (multiply, 0, 1, 2),
+            (multiply, 0, 0, 3), (multiply, 0, 0, 2), (magnitude, 0, 1, 1), (transform_x, 0, 0, 1),
+            (transform_x, 0, 1, 3), (quantize_signal, "x", 1, 0), (turn, "v", 1, 0),
+            (add_filter, 0, 0, 1, nc.gpsimd.tensor_tensor), (interleave, "x", 1, 1, 0, nc.scalar.copy),
+            (turn, "v", 1, 1), (add_filter, 0, 1, 3, nc.vector.tensor_tensor), (multiply, 0, 0, 1),
+            (multiply, 0, 1, 3), (quantize_signal, "z", 1, 1), (transform_z, 1, 0, 0), (magnitude, 0, 1, 0),
+            (gate, 0, 1, 0), (transform_z, 1, 1, 0), (quantize_product, 0, 0, 0), (transform_x, 0, 1, 1),
+            (quantize_product, 0, 1, 1), (unpack, "v", 1, 0), (quantize_weight, "v", 0, 0),
+            (add_filter, 0, 1, 1, nc.gpsimd.tensor_tensor), (transform_x, 0, 1, 0),
+            (quantize_product, 0, 0, 1), (interleave, "x", 1, 1, 1, nc.vector.tensor_copy),
+            (add_filter, 0, 1, 0, nc.vector.tensor_tensor), (transform_z, 1, 0, 1), (magnitude, 1, 1, 0),
+            (quantize_weight, "v", 0, 1), (unpack, "v", 1, 1), (magnitude, 1, 0, 0), (gate, 0, 0, 0),
+            (magnitude, 1, 0, 1), (multiply, 0, 1, 1), (multiply, 0, 1, 0), (transform_back, 0, 0, 1, 0),
+            (add_filter, 1, 1, 0, nc.gpsimd.tensor_tensor), (quantize_signal, "x", 1, 1),
+            (transform_back, 0, 0, 1, 1), (add_filter, 1, 0, 1, nc.gpsimd.tensor_tensor),
+            (quantize_product, 0, 1, 0), (gate, 1, 1, 0), (transform_z, 1, 1, 2), (transform_x, 1, 1, 0),
+            (quantize_weight, "v", 1, 0), (magnitude, 1, 1, 2), (quantize_weight, "v", 1, 1), (gate, 0, 0, 1),
+            (transform_x, 1, 0, 0), (multiply, 1, 1, 0), (apply_gate, 0, 0, 1, 0), (gate, 0, 1, 1),
+            (transform_back, 0, 0, 0, 1), (transform_back, 0, 0, 0, 0), (transform_x, 1, 0, 1),
+            (transform_z, 1, 1, 1), (apply_gate, 0, 0, 0, 0), (magnitude, 1, 1, 1),
+            (transform_back, 0, 1, 0, 0), (apply_gate, 0, 0, 0, 1), (transform_back, 0, 1, 1, 0),
+            (add_filter, 1, 0, 0, nc.gpsimd.tensor_tensor), (regroup, 0, 0, 0, nc.scalar.copy),
+            (multiply, 1, 0, 1), (transform_z, 1, 1, 3), (transform_z, 1, 0, 2), (multiply, 1, 0, 0),
+            (apply_gate, 0, 0, 1, 1), (add_filter, 1, 1, 2, nc.gpsimd.tensor_tensor),
+            (transform_back, 0, 1, 1, 1), (transform_x, 1, 1, 1), (transform_back, 0, 1, 0, 1),
+            (add_filter, 1, 1, 1, nc.gpsimd.tensor_tensor), (apply_gate, 0, 1, 0, 0), (magnitude, 1, 1, 3),
+            (store_result, 0, 0, 0), (quantize_result, 0, 0, 0), (quantize_product, 1, 0, 0),
+            (transform_x, 1, 1, 3), (apply_gate, 0, 1, 1, 0), (transform_z, 1, 0, 3),
+            (regroup, 0, 0, 1, nc.scalar.copy), (apply_gate, 0, 1, 1, 1), (multiply, 1, 1, 1),
+            (magnitude, 1, 0, 2), (store_codes, 0, 0, 0), (quantize_result, 0, 0, 1),
+            (regroup, 0, 1, 1, nc.scalar.copy), (add_filter, 1, 1, 3, nc.gpsimd.tensor_tensor),
+            (apply_gate, 0, 1, 0, 1), (multiply, 1, 1, 3), (add_filter, 1, 0, 2, nc.gpsimd.tensor_tensor),
+            (store_result, 0, 0, 1), (transform_x, 1, 1, 2), (magnitude, 1, 0, 3), (quantize_result, 0, 1, 1),
+            (transform_x, 1, 0, 2), (gate, 1, 1, 1), (regroup, 0, 1, 0, nc.scalar.copy),
+            (add_filter, 1, 0, 3, nc.gpsimd.tensor_tensor), (quantize_product, 1, 1, 0), (multiply, 1, 1, 2),
+            (transform_back, 1, 1, 0, 0), (transform_x, 1, 0, 3), (gate, 1, 0, 0), (multiply, 1, 0, 2),
+            (transform_back, 1, 1, 0, 1), (apply_gate, 1, 1, 0, 0), (quantize_product, 1, 1, 1),
+            (multiply, 1, 0, 3), (transform_back, 1, 0, 0, 0), (quantize_result, 0, 1, 0),
+            (transform_back, 1, 0, 0, 1), (quantize_product, 1, 0, 1), (store_result, 0, 1, 1),
+            (apply_gate, 1, 1, 0, 1), (transform_back, 1, 1, 1, 0), (gate, 1, 0, 1), (store_codes, 0, 0, 1),
+            (store_result, 0, 1, 0), (store_codes, 0, 1, 0), (transform_back, 1, 0, 1, 0),
+            (apply_gate, 1, 0, 0, 0), (regroup, 1, 1, 0, nc.scalar.copy), (transform_back, 1, 1, 1, 1),
+            (apply_gate, 1, 0, 0, 1), (store_codes, 0, 1, 1), (transform_back, 1, 0, 1, 1),
+            (regroup, 1, 0, 0, nc.scalar.copy), (store_result, 1, 1, 0), (apply_gate, 1, 1, 1, 0),
+            (apply_gate, 1, 1, 1, 1), (store_result, 1, 0, 0), (apply_gate, 1, 0, 1, 0),
+            (apply_gate, 1, 0, 1, 1), (store_result, 1, 1, 1), (store_result, 1, 0, 1),
+            (regroup, 1, 1, 1, nc.scalar.copy), (quantize_result, 1, 1, 0), (store_codes, 1, 1, 0),
+            (regroup, 1, 0, 1, nc.vector.tensor_copy), (quantize_result, 1, 1, 1), (quantize_result, 1, 0, 1),
+            (quantize_result, 1, 0, 0), (store_codes, 1, 1, 1), (store_codes, 1, 0, 1), (store_scales,),
+            (store_codes, 1, 0, 0),
+        ]
+
+        for step, *arguments in loads + work:
+            step(*arguments)

from contextlib import ExitStack

import concourse.mybir as mybir
from concourse.masks import make_identity

F32 = mybir.dt.float32
BF16 = mybir.dt.bfloat16
U32 = mybir.dt.uint32
I32 = mybir.dt.int32
U8 = mybir.dt.uint8
FP8X4 = mybir.dt.float8_e4m3fn_x4
ACT = mybir.ActivationFunctionType
ALU = mybir.AluOpType

B, N, M, C = 2, 1024, 1024, 512
FLOPS = 3 * 2 * B * N * M * C

P = 128
T = 4
GROUP = P * T
NG = N // GROUP
CHUNK = P
HALF = C // 2
SCALE_ROWS = 4


def tile_orchiddatadependentspectralconv_x1_kernel(tc, x, z, q, u, uh, h0, v, out_0, out_1, out_2):
    nc = tc.nc
    signals = {"x": x, "z": z}
    weights = {"u": u, "uh": uh, "v": v}

    with ExitStack() as ctx:
        keep = ctx.enter_context(tc.tile_pool(name="keep", bufs=1))
        weight_pool = ctx.enter_context(tc.tile_pool(name="weight_pool", bufs=4))
        signal_pool = ctx.enter_context(tc.tile_pool(name="signal_pool", bufs=4))
        gate_in_pool = ctx.enter_context(tc.tile_pool(name="gate_in_pool", bufs=4))
        group_pool = ctx.enter_context(tc.tile_pool(name="group_pool", bufs=3))
        result_pool = ctx.enter_context(tc.tile_pool(name="result_pool", bufs=2))
        gate_pool = ctx.enter_context(tc.tile_pool(name="gate_pool", bufs=3))
        filter_pool = ctx.enter_context(tc.tile_pool(name="filter_pool", bufs=3))
        psum = ctx.enter_context(tc.psum_pool(name="psum", bufs=2))

        ctx.enter_context(tc.manual_schedule())

        ident = keep.tile([P, P], F32, name="ident")
        make_identity(nc, ident[:])
        zero = keep.tile([P, 1], F32, name="zero")
        nc.vector.memset(zero[:], 0.0)
        nc.scalar.activation(out=zero[:], in_=zero[:], func=ACT.Silu)

        filters = keep.tile([P, NG, T, C], BF16, name="filters")
        out_scales = keep.tile([P, NG, B * C], U8, align_bytes=64, name="out_scales")

        raw = {}
        grouped = {}
        codes, scales = {}, {}
        banks = {}
        live = {}
        out_codes = {}

        def row_words(rows):
            return rows.rearrange("(p t) c -> p t c", t=T)

        def block(g):
            return slice(g * GROUP, (g + 1) * GROUP)

        def half_columns(half):
            return slice(half * HALF, (half + 1) * HALF)

        def by_fours(tile_view):
            return tile_view.rearrange("p (c i) t -> p c t i", i=4)

        def by_fours_of_rows(tile_view):
            return tile_view.rearrange("p t (c i) -> p c t i", i=4)

        def load_weight(w, g, pair):
            if (w, g) not in raw:
                raw[w, g] = weight_pool.tile([P, T, N], BF16, name="weight_in")
            ts = slice(2 * pair, 2 * pair + 2)
            nc.sync.dma_start(out=raw[w, g][:, ts, :], in_=row_words(weights[w][block(g), :])[:, ts, :])

        def load_signal(s, b, k):
            raw[s, b, k] = signal_pool.tile([P, T, C], BF16, name="signal_in")
            nc.sync.dma_start(out=raw[s, b, k][:], in_=row_words(signals[s][b, block(k), :]))

        def load_filter(g):
            nc.sync.dma_start(out=filters[:, g, :, :], in_=row_words(h0[block(g), :]))

        def load_gate(b, g):
            raw["q", b, g] = gate_in_pool.tile([P, T, C], BF16, name="gate_in")
            nc.sync.dma_start(out=raw["q", b, g][:], in_=row_words(q[b, block(g), :]))

        def quantize(key, k, columns, grouped_tile):
            if key not in codes:
                codes[key] = keep.tile([P, NG, GROUP], U32, align_bytes=64, name="codes_%s_%d" % key)
                scales[key] = keep.tile([P, NG, GROUP], U8, align_bytes=64, name="scales_%s_%d" % key)
            nc.vector.quantize_mx(
                out=codes[key][:, k, columns].bitcast(FP8X4),
                scales=scales[key][:, k, columns],
                in_=grouped_tile[:, columns, :].rearrange("p w t -> p (w t)"),
            )

        def turn(w, g, pair):
            words = raw[w, g][:].bitcast(F32)
            for k in range(NG):
                bank = psum.tile([P, 2, 2, P], F32, name="turned", tag="bank", bufs=4)
                banks[w, g, pair, k] = bank
                for t in range(2):
                    for e in range(2):
                        nc.tensor.transpose(
                            bank[:, t, e, :], words[:, 2 * pair + t, 2 * P * k + e : 2 * P * (k + 1) : 2], ident[:]
                        )

        def unpack(w, g, pair):
            for k in range(NG):
                if (w, g, k) not in grouped:
                    grouped[w, g, k] = group_pool.tile([P, GROUP, T], BF16, align_bytes=64, name="weight_grouped", bufs=4)
                words = grouped[w, g, k][:].rearrange("p w t -> p (w t)").bitcast(F32)
                nc.scalar.copy(
                    out=words[:, pair * GROUP : (pair + 1) * GROUP].rearrange("p (t m e) -> p t m e", t=2, e=2),
                    in_=banks[w, g, pair, k][:].rearrange("p t e m -> p t m e"),
                )

        def quantize_weight(w, g, k):
            quantize((w, g), k, slice(0, GROUP), grouped[w, g, k])

        def interleave(s, b, k, half, copy):
            if (s, b, k) not in grouped:
                grouped[s, b, k] = group_pool.tile([P, C, T], BF16, align_bytes=64, name="signal_grouped")
            columns = half_columns(half)
            copy(
                out=by_fours(grouped[s, b, k][:, columns, :]), in_=by_fours_of_rows(raw[s, b, k][:, :, columns])
            )

        def quantize_signal(s, b, k):
            quantize((s, b), k, slice(0, C), grouped[s, b, k])

        def multiply_mx(out, weight, t, moving, columns):
            rows = slice(t * P, (t + 1) * P)
            for k in range(NG):
                nc.tensor.matmul_mx(
                    out=out,
                    lhsT=codes[weight][:, k, rows].bitcast(FP8X4),
                    lhsT_scale=scales[weight][:, k, rows],
                    rhs=codes[moving][:, k, columns].bitcast(FP8X4),
                    rhs_scale=scales[moving][:, k, columns],
                    start=(k == 0),
                    stop=(k == NG - 1),
                )

        def chunk_columns(c):
            return slice(c * CHUNK, (c + 1) * CHUNK)

        def transform(name, b, g, c, w, s):
            banks[name, b, g, c] = psum.tile([P, T, CHUNK], F32, name=name)
            for t in range(T):
                multiply_mx(banks[name, b, g, c][:, t, :], (w, g), t, (s, b), chunk_columns(c))

        def transform_z(b, g, c):
            transform("zs", b, g, c, "uh", "z")

        def transform_x(b, g, c):
            transform("xs", b, g, c, "u", "x")

        def magnitude(b, g, c):
            live["mag", b, g, c] = filter_pool.tile([P, T, CHUNK], F32, name="mag")
            nc.scalar.activation(out=live["mag", b, g, c][:], in_=banks["zs", b, g, c][:], func=ACT.Abs)

        def add_filter(b, g, c, tensor_tensor):
            live["h", b, g, c] = filter_pool.tile([P, T, CHUNK], F32, name="h")
            tensor_tensor(
                out=live["h", b, g, c][:],
                in0=live["mag", b, g, c][:],
                in1=filters[:, g, :, chunk_columns(c)],
                op=ALU.add,
            )

        def multiply(b, g, c):
            if ("p", b, g) not in grouped:
                grouped["p", b, g] = result_pool.tile([P, C, T], BF16, align_bytes=64, name="p_grouped")
            nc.vector.tensor_tensor(
                out=by_fours(grouped["p", b, g][:, chunk_columns(c), :]),
                in0=by_fours_of_rows(banks["xs", b, g, c][:]),
                in1=by_fours_of_rows(live["h", b, g, c][:]),
                op=ALU.mult,
            )

        def quantize_product(b, g, half):
            quantize(("p", b), g, half_columns(half), grouped["p", b, g])

        def gate(b, g, pair):
            if ("gate", b, g) not in live:
                live["gate", b, g] = gate_pool.tile([P, T, C], F32, name="gate")
            ts = slice(2 * pair, 2 * pair + 2)
            nc.scalar.activation(
                out=live["gate", b, g][:, ts, :], in_=raw["q", b, g][:, ts, :], func=ACT.Silu, bias=zero[:]
            )

        def transform_back(b, g, half, pair):
            banks["r", b, g, half, pair] = psum.tile([P, 2, HALF], F32, name="r", tag="bank", bufs=4)
            for t in range(2):
                out = banks["r", b, g, half, pair][:, t, :]
                multiply_mx(out, ("v", g), 2 * pair + t, ("p", b), half_columns(half))

        def apply_gate(b, g, half, pair):
            if ("out", b, g) not in live:
                live["out", b, g] = result_pool.tile([P, T, C], F32, name="result")
            ts = slice(2 * pair, 2 * pair + 2)
            nc.vector.tensor_tensor(
                out=live["out", b, g][:, ts, half_columns(half)],
                in0=banks["r", b, g, half, pair][:],
                in1=live["gate", b, g][:, ts, half_columns(half)],
                op=ALU.mult,
            )

        def store_result(b, g, half):
            columns = half_columns(half)
            nc.sync.dma_start(out=row_words(out_0[b, block(g), columns]), in_=live["out", b, g][:, :, columns])

        def regroup(b, g, half, copy):
            if ("out", b, g) not in grouped:
                grouped["out", b, g] = result_pool.tile([P, C, T], BF16, align_bytes=64, name="out_grouped")
            columns = half_columns(half)
            copy(
                out=by_fours(grouped["out", b, g][:, columns, :]),
                in_=by_fours_of_rows(live["out", b, g][:, :, columns]),
            )

        def quantize_result(b, g, half):
            if (b, g) not in out_codes:
                out_codes[b, g] = result_pool.tile([P, C], U32, align_bytes=64, name="out_codes")
            columns = half_columns(half)
            first = b * C + half * HALF
            nc.vector.quantize_mx(
                out=out_codes[b, g][:, columns].bitcast(FP8X4),
                scales=out_scales[:, g, first : first + HALF],
                in_=grouped["out", b, g][:, columns, :].rearrange("p w t -> p (w t)"),
            )

        def store_codes(b, g, half):
            first = b * C + half * HALF
            nc.sync.dma_start(
                out=out_1[g, :, first : first + HALF, :].bitcast(I32).rearrange("p c o -> p (c o)"),
                in_=out_codes[b, g][:, half_columns(half)].bitcast(I32),
            )

        def store_scales():
            for j in range(P // 32):
                nc.scalar.dma_start(
                    out=out_2[:, SCALE_ROWS * j : SCALE_ROWS * (j + 1), :].bitcast(I32).rearrange("g r m -> r g m"),
                    in_=out_scales[32 * j : 32 * j + SCALE_ROWS, :, :].bitcast(I32),
                )

        loads = [
            (load_signal, "z", 0, 0), (load_signal, "z", 0, 1), (load_weight, "uh", 0, 0),
            (load_weight, "uh", 0, 1), (load_weight, "u", 0, 0), (load_weight, "u", 0, 1),
            (load_signal, "x", 0, 0), (load_weight, "uh", 1, 0), (load_weight, "uh", 1, 1),
            (load_signal, "z", 1, 0), (load_signal, "x", 0, 1), (load_weight, "u", 1, 0),
            (load_weight, "u", 1, 1), (load_filter, 0), (load_weight, "v", 0, 0), (load_weight, "v", 0, 1),
            (load_signal, "x", 1, 0), (load_filter, 1), (load_signal, "z", 1, 1), (load_signal, "x", 1, 1),
            (load_gate, 0, 1), (load_weight, "v", 1, 0), (load_weight, "v", 1, 1), (load_gate, 1, 0),
            (load_gate, 1, 1), (load_gate, 0, 0),
        ]

        work = [
            (interleave, "z", 0, 0, 0, nc.vector.tensor_copy),
            (interleave, "z", 0, 1, 0, nc.vector.tensor_copy),
            (interleave, "z", 0, 0, 1, nc.vector.tensor_copy), (turn, "uh", 0, 0), (unpack, "uh", 0, 0),
            (interleave, "z", 0, 1, 1, nc.vector.tensor_copy), (turn, "uh", 0, 1), (unpack, "uh", 0, 1),
            (quantize_signal, "z", 0, 1), (turn, "u", 0, 0), (quantize_signal, "z", 0, 0),
            (quantize_weight, "uh", 0, 0), (quantize_weight, "uh", 0, 1), (turn, "u", 0, 1),
            (interleave, "x", 0, 0, 0, nc.vector.tensor_copy), (unpack, "u", 0, 0),
            (interleave, "x", 0, 0, 1, nc.vector.tensor_copy), (transform_z, 0, 0, 0), (unpack, "u", 0, 1),
            (transform_z, 0, 0, 2), (quantize_weight, "u", 0, 0),
            (interleave, "z", 1, 0, 0, nc.vector.tensor_copy), (magnitude, 0, 0, 0),
            (quantize_signal, "x", 0, 0), (turn, "uh", 1, 0), (quantize_weight, "u", 0, 1),
            (interleave, "x", 0, 1, 0, nc.vector.tensor_copy), (turn, "uh", 1, 1), (transform_z, 0, 0, 3),
            (magnitude, 0, 0, 2), (unpack, "uh", 1, 0), (transform_z, 0, 0, 1), (unpack, "uh", 1, 1),
            (turn, "u", 1, 0), (interleave, "x", 0, 1, 1, nc.scalar.copy), (quantize_weight, "uh", 1, 0),
            (quantize_weight, "uh", 1, 1), (turn, "u", 1, 1), (transform_z, 0, 1, 2), (turn, "v", 0, 0),
            (magnitude, 0, 0, 1), (quantize_signal, "x", 0, 1), (add_filter, 0, 0, 0, nc.vector.tensor_tensor),
            (unpack, "u", 1, 0), (magnitude, 0, 0, 3), (turn, "v", 0, 1),
            (interleave, "z", 1, 0, 1, nc.vector.tensor_copy), (unpack, "u", 1, 1),
            (add_filter, 0, 0, 3, nc.vector.tensor_tensor), (unpack, "v", 0, 0), (quantize_signal, "z", 1, 0),
            (magnitude, 0, 1, 2), (quantize_weight, "u", 1, 0), (quantize_weight, "u", 1, 1),
            (add_filter, 0, 1, 2, nc.gpsimd.tensor_tensor), (transform_x, 0, 0, 0), (transform_z, 0, 1, 0),
            (interleave, "x", 1, 0, 0, nc.vector.tensor_copy), (interleave, "x", 1, 0, 1, nc.scalar.copy),
            (transform_x, 0, 1, 2), (interleave, "z", 1, 1, 0, nc.scalar.copy), (transform_z, 0, 1, 3),
            (multiply, 0, 0, 0), (transform_x, 0, 0, 3), (magnitude, 0, 1, 3),
            (interleave, "z", 1, 1, 1, nc.vector.tensor_copy), (add_filter, 0, 0, 2, nc.gpsimd.tensor_tensor),
            (unpack, "v", 0, 1), (transform_x, 0, 0, 2), (transform_z, 0, 1, 1), (multiply, 0, 1, 2),
            (multiply, 0, 0, 3), (multiply, 0, 0, 2), (magnitude, 0, 1, 1), (transform_x, 0, 0, 1),
            (transform_x, 0, 1, 3), (quantize_signal, "x", 1, 0), (turn, "v", 1, 0),
            (add_filter, 0, 0, 1, nc.gpsimd.tensor_tensor), (interleave, "x", 1, 1, 0, nc.scalar.copy),
            (turn, "v", 1, 1), (add_filter, 0, 1, 3, nc.vector.tensor_tensor), (multiply, 0, 0, 1),
            (multiply, 0, 1, 3), (quantize_signal, "z", 1, 1), (transform_z, 1, 0, 0), (magnitude, 0, 1, 0),
            (gate, 0, 1, 0), (transform_z, 1, 1, 0), (quantize_product, 0, 0, 0), (transform_x, 0, 1, 1),
            (quantize_product, 0, 1, 1), (unpack, "v", 1, 0), (quantize_weight, "v", 0, 0),
            (add_filter, 0, 1, 1, nc.gpsimd.tensor_tensor), (transform_x, 0, 1, 0),
            (quantize_product, 0, 0, 1), (interleave, "x", 1, 1, 1, nc.vector.tensor_copy),
            (add_filter, 0, 1, 0, nc.vector.tensor_tensor), (transform_z, 1, 0, 1), (magnitude, 1, 1, 0),
            (quantize_weight, "v", 0, 1), (unpack, "v", 1, 1), (magnitude, 1, 0, 0), (gate, 0, 0, 0),
            (magnitude, 1, 0, 1), (multiply, 0, 1, 1), (multiply, 0, 1, 0), (transform_back, 0, 0, 1, 0),
            (add_filter, 1, 1, 0, nc.gpsimd.tensor_tensor), (quantize_signal, "x", 1, 1),
            (transform_back, 0, 0, 1, 1), (add_filter, 1, 0, 1, nc.gpsimd.tensor_tensor),
            (quantize_product, 0, 1, 0), (gate, 1, 1, 0), (transform_z, 1, 1, 2), (transform_x, 1, 1, 0),
            (quantize_weight, "v", 1, 0), (magnitude, 1, 1, 2), (quantize_weight, "v", 1, 1), (gate, 0, 0, 1),
            (transform_x, 1, 0, 0), (multiply, 1, 1, 0), (apply_gate, 0, 0, 1, 0), (gate, 0, 1, 1),
            (transform_back, 0, 0, 0, 1), (transform_back, 0, 0, 0, 0), (transform_x, 1, 0, 1),
            (transform_z, 1, 1, 1), (apply_gate, 0, 0, 0, 0), (magnitude, 1, 1, 1),
            (transform_back, 0, 1, 0, 0), (apply_gate, 0, 0, 0, 1), (transform_back, 0, 1, 1, 0),
            (add_filter, 1, 0, 0, nc.gpsimd.tensor_tensor), (regroup, 0, 0, 0, nc.scalar.copy),
            (multiply, 1, 0, 1), (transform_z, 1, 1, 3), (transform_z, 1, 0, 2), (multiply, 1, 0, 0),
            (apply_gate, 0, 0, 1, 1), (add_filter, 1, 1, 2, nc.gpsimd.tensor_tensor),
            (transform_back, 0, 1, 1, 1), (transform_x, 1, 1, 1), (transform_back, 0, 1, 0, 1),
            (add_filter, 1, 1, 1, nc.gpsimd.tensor_tensor), (apply_gate, 0, 1, 0, 0), (magnitude, 1, 1, 3),
            (store_result, 0, 0, 0), (quantize_result, 0, 0, 0), (quantize_product, 1, 0, 0),
            (transform_x, 1, 1, 3), (apply_gate, 0, 1, 1, 0), (transform_z, 1, 0, 3),
            (regroup, 0, 0, 1, nc.scalar.copy), (apply_gate, 0, 1, 1, 1), (multiply, 1, 1, 1),
            (magnitude, 1, 0, 2), (store_codes, 0, 0, 0), (quantize_result, 0, 0, 1),
            (regroup, 0, 1, 1, nc.scalar.copy), (add_filter, 1, 1, 3, nc.gpsimd.tensor_tensor),
            (apply_gate, 0, 1, 0, 1), (multiply, 1, 1, 3), (add_filter, 1, 0, 2, nc.gpsimd.tensor_tensor),
            (store_result, 0, 0, 1), (transform_x, 1, 1, 2), (magnitude, 1, 0, 3), (quantize_result, 0, 1, 1),
            (transform_x, 1, 0, 2), (gate, 1, 1, 1), (regroup, 0, 1, 0, nc.scalar.copy),
            (add_filter, 1, 0, 3, nc.gpsimd.tensor_tensor), (quantize_product, 1, 1, 0), (multiply, 1, 1, 2),
            (transform_back, 1, 1, 0, 0), (transform_x, 1, 0, 3), (gate, 1, 0, 0), (multiply, 1, 0, 2),
            (transform_back, 1, 1, 0, 1), (apply_gate, 1, 1, 0, 0), (quantize_product, 1, 1, 1),
            (multiply, 1, 0, 3), (transform_back, 1, 0, 0, 0), (quantize_result, 0, 1, 0),
            (transform_back, 1, 0, 0, 1), (quantize_product, 1, 0, 1), (store_result, 0, 1, 1),
            (apply_gate, 1, 1, 0, 1), (transform_back, 1, 1, 1, 0), (gate, 1, 0, 1), (store_codes, 0, 0, 1),
            (store_result, 0, 1, 0), (store_codes, 0, 1, 0), (transform_back, 1, 0, 1, 0),
            (apply_gate, 1, 0, 0, 0), (regroup, 1, 1, 0, nc.scalar.copy), (transform_back, 1, 1, 1, 1),
            (apply_gate, 1, 0, 0, 1), (store_codes, 0, 1, 1), (transform_back, 1, 0, 1, 1),
            (regroup, 1, 0, 0, nc.scalar.copy), (store_result, 1, 1, 0), (apply_gate, 1, 1, 1, 0),
            (apply_gate, 1, 1, 1, 1), (store_result, 1, 0, 0), (apply_gate, 1, 0, 1, 0),
            (apply_gate, 1, 0, 1, 1), (store_result, 1, 1, 1), (store_result, 1, 0, 1),
            (regroup, 1, 1, 1, nc.scalar.copy), (quantize_result, 1, 1, 0), (store_codes, 1, 1, 0),
            (regroup, 1, 0, 1, nc.vector.tensor_copy), (quantize_result, 1, 1, 1), (quantize_result, 1, 0, 1),
            (quantize_result, 1, 0, 0), (store_codes, 1, 1, 1), (store_codes, 1, 0, 1), (store_scales,),
            (store_codes, 1, 0, 0),
        ]

        for step, *arguments in loads + work:
            step(*arguments)
